import numpy as np
import ml_dtypes


def mxq(x, axis, fmt="e4m3"):
    dtype, down = {"e4m3": (ml_dtypes.float8_e4m3fn, 7), "e5m2": (ml_dtypes.float8_e5m2, 14)}[fmt]
    v = np.moveaxis(np.asarray(x, np.float32).astype(ml_dtypes.bfloat16).astype(np.float64), axis, -1)
    blocks = v.reshape(v.shape[:-1] + (-1, 32))
    amax = np.abs(blocks).max(-1, keepdims=True)
    byte = np.maximum(np.where(amax > 0, np.frexp(amax)[1] - 1 + 127, 0) - down, 1)
    scale = np.exp2(byte - 127.0)
    codes = (blocks / scale).astype(np.float32).astype(dtype).astype(np.float64)
    return np.moveaxis((codes * scale).reshape(v.shape), -1, axis)


WIDE = False


def mx_kscale(k):
    if not WIDE:
        return np.ones(k)
    levels = np.array([10, -10, 5, -5, 0])
    if k % 512:
        return np.exp2(np.random.permutation(np.resize(levels, k // 32))).repeat(32)
    a = np.empty((k // 512, 16))
    for p in range(k // 512):
        a[p, :8] = np.random.permutation(np.resize(levels, 8))
        for g in range(8):
            far = levels[np.abs(levels - a[p, g]) >= 10]
            a[p, g + 8] = far[np.random.randint(len(far))]
    return np.exp2(a.ravel()).repeat(32)


def f64(x):
    return np.asarray(x).astype(np.float64)


def striped(idx):
    return np.tile(idx.reshape(-1, 16).T, (8, 1)).astype(np.uint16)


def unstriped(offs):
    return offs[:16].T.reshape(-1).astype(np.int64)


E2M1 = np.array([0.0, 0.5, 1.0, 1.5, 2.0, 3.0, 4.0, 6.0, -0.0, -0.5, -1.0, -1.5, -2.0, -3.0, -4.0, -6.0])


def pack_weight(w, fmt):
    k, n = w.shape
    w = f64(np.asarray(w, np.float32).astype(ml_dtypes.bfloat16)).reshape(k // 32, 32, n)
    amax = np.abs(w).max(1)
    if fmt == "e4m3":
        byte = np.frexp(amax)[1] - 1 + 127 - 7
    else:
        mant, ex = np.frexp(amax / 6.0)
        byte = np.where(mant > 0.5, ex, ex - 1) + 127
    byte = np.clip(np.where(amax > 0, byte, 1), 1, 254)
    scaled = (w * np.exp2(127.0 - byte)[:, None, :]).reshape(k, n).astype(np.float32)
    by_word = np.ascontiguousarray(scaled.reshape(k // 512, 128, 4, n).transpose(0, 1, 3, 2))
    if fmt == "e4m3":
        words = by_word.astype(ml_dtypes.float8_e4m3fn).view(np.uint8)
    else:
        c = by_word.astype(ml_dtypes.float4_e2m1fn).view(np.uint8) & 0xF
        words = (c[..., 0::2] | (c[..., 1::2] << 4)).reshape(k // 512, 128, 2 * n)
    return np.ascontiguousarray(words), np.ascontiguousarray(byte.astype(np.uint8).reshape(k // 512, 16, n))


def unpack_weight(words, scales, fmt):
    g, _, n = scales.shape
    words = np.ascontiguousarray(words).reshape(g, 128, n, -1)
    if fmt == "e4m3":
        vals = words.view(ml_dtypes.float8_e4m3fn).astype(np.float64)
    else:
        nib = np.empty((g, 128, n, 4), np.uint8)
        nib[..., 0::2] = words & 0xF
        nib[..., 1::2] = words >> 4
        vals = E2M1[nib]
    vals = vals * np.repeat(np.exp2(scales.astype(np.float64) - 127.0), 8, axis=1)[..., None]
    return vals.transpose(0, 1, 3, 2).reshape(g * 512, n)


def gelu(v):
    return 0.5 * v * (1.0 + np.tanh(np.sqrt(2.0 / np.pi) * (v + 0.044715 * v**3)))


def striped8(idx):
    return np.concatenate([v.reshape(-1, 16).T for v in idx]).astype(np.uint16)


def unstriped8(offs):
    return np.stack([offs[16 * g:16 * g + 16].T.reshape(-1) for g in range(8)]).astype(np.int64)


def heads(h, wgt, idx8):
    r = np.arange(h.shape[0])
    return wgt[r // 4 % 128] * h[r[:, None], idx8[r % 512 // 64]]


T, S, P, K, H, N = 4096, 1024, 512, 512, 1024, 768

def setup_inputs():
    n = np.random.standard_normal
    s = mx_kscale(K)[:, None]
    u = mx_kscale(H)[:, None]
    tab_words, tab_scales = pack_weight(n((K, T)) * s, "e4m3")
    wb_words, wb_scales = pack_weight(n((K, H)) / np.sqrt(K) / s * u.T, "e2m1")
    wo_words, wo_scales = pack_weight(n((H, N)) / np.sqrt(H) / u, "e4m3")
    angle = np.random.uniform(-3.0, 3.0, (H, P))
    return {
        "tab_words": tab_words, "tab_scales": tab_scales,
        "offs": striped(np.random.permutation(T)[:S]),
        "offs2": striped8(np.stack([np.random.permutation(S)[:P] for _ in range(8)])),
        "wa": (n((K, H)) / np.sqrt(K) / s * u.T).astype(np.float32),
        "wb_words": wb_words, "wb_scales": wb_scales,
        "wgt": np.repeat(np.random.uniform(0.5, 2.0, (8, P)), 16, axis=0).astype(np.float32),
        "cosm": np.cos(angle).astype(np.float32),
        "sinm": np.sin(angle).astype(np.float32),
        "wo_words": wo_words, "wo_scales": wo_scales,
    }

def reference(tab_words, tab_scales, offs, offs2, wa, wb_words, wb_scales, wgt, cosm, sinm, wo_words, wo_scales):
    v = unpack_weight(tab_words, tab_scales, "e4m3")[:, unstriped(offs)]
    wb = unpack_weight(wb_words, wb_scales, "e2m1")
    wo = unpack_weight(wo_words, wo_scales, "e4m3")
    ha = mxq(f64(wa), 0, "e4m3").T @ v
    hb = wb.T @ v
    xa = heads(ha, f64(wgt), unstriped8(offs2))
    xb = heads(hb, f64(wgt), unstriped8(offs2))
    z = xa * f64(cosm) + xb * f64(sinm)
    return wo.T @ mxq(z, 0, "e4m3")

@@ -1,0 +1,246 @@
+from contextlib import ExitStack
+
+import concourse.mybir as mybir
+from concourse.masks import make_identity
+
+T, S, M, K, H, N = 4096, 1024, 512, 512, 1024, 768
+FLOPS = 2 * K * H * S * 2 + 2 * H * N * M
+
+F32 = mybir.dt.float32
+BF16 = mybir.dt.bfloat16
+I32 = mybir.dt.int32
+U32 = mybir.dt.uint32
+U16 = mybir.dt.uint16
+U8 = mybir.dt.uint8
+FP8X4 = mybir.dt.float8_e4m3fn_x4
+FP4X4 = mybir.dt.float4_e2m1fn_x4
+MULT = mybir.AluOpType.mult
+
+P = 128
+BANK = 512
+HALF = 256
+
+
+def tile_list_latent_key_rebuild_kernel(
+    tc, tab_words, tab_scales, offs, offs2, wa, wb_words, wb_scales, wgt, cosm, sinm, wo_words, wo_scales, out
+):
+    nc = tc.nc
+    with ExitStack() as ctx:
+        keep = ctx.enter_context(tc.tile_pool(name="keep", bufs=1))
+        hpool = ctx.enter_context(tc.tile_pool(name="hpool", bufs=6))
+        psum = ctx.enter_context(tc.psum_pool(name="psum", bufs=1))
+
+        def held(name, shape, dtype):
+            return keep.tile(shape, dtype, name=name, align_bytes=64)
+
+        offs_t = keep.tile([P, S // 16], U16, name="offs_t")
+        offs2_t = keep.tile([P, M // 16], U16, name="offs2_t")
+        tab_w = held("tab_w", [P, T], U32)
+        tab_s = held("tab_s", [P, T], U8)
+        wb_w = held("wb_w", [P, 2 * H], U8)
+        wb_s = held("wb_s", [P, H], U8)
+        wo_w = [held("wo_w%d" % b, [P, N], U32) for b in range(2)]
+        wo_s = held("wo_s", [P, 2, N], U8)
+        wa_raw = [held("wa_raw%d" % b, [P, 4, BANK], F32) for b in range(2)]
+        wgt_t = held("wgt_t", [P, M], F32)
+        cos_t = [[held("cos%d%d" % (b, u), [P, 2, M], F32) for u in range(2)] for b in range(2)]
+        sin_t = [[held("sin%d%d" % (b, u), [P, 2, M], F32) for u in range(2)] for b in range(2)]
+        ident = held("ident", [P, P], F32)
+
+        nc.vector.memset(tab_s[:].bitcast(I32), 0)
+        nc.vector.memset(wb_s[:].bitcast(I32), 0)
+        nc.vector.memset(wo_s[:].rearrange("p b n -> p (b n)").bitcast(I32), 0)
+        make_identity(nc, ident[:])
+
+        tab_rows = tab_words[0].rearrange("p t i -> p (t i)").bitcast(I32)
+        wa_rows = wa.rearrange("(p j) r -> p j r", j=4)
+        cos_rows = cosm.rearrange("(b p i) m -> b p i m", b=2, i=4)
+        sin_rows = sinm.rearrange("(b p i) m -> b p i m", b=2, i=4)
+
+        def load_angles(tiles, rows, b, u):
+            nc.sync.dma_start(tiles[b][u][:], rows[b, :, 2 * u : 2 * u + 2, :])
+
+        first = T // 4
+        nc.sync.dma_start(offs_t[:], offs)
+        nc.sync.dma_start(wb_w[:].bitcast(I32), wb_words[0].bitcast(I32))
+        nc.sync.dma_start(tab_w[:, :first].bitcast(I32), tab_rows[:, :first])
+        for q in range(4):
+            nc.sync.dma_start(
+                tab_s[32 * q : 32 * q + 4, :].bitcast(I32), tab_scales[0, 4 * q : 4 * q + 4, :].bitcast(I32)
+            )
+        nc.sync.dma_start(tab_w[:, first:].bitcast(I32), tab_rows[:, first:])
+        for q in range(4):
+            nc.scalar.dma_start(
+                wb_s[32 * q : 32 * q + 4, :].bitcast(I32), wb_scales[0, 4 * q : 4 * q + 4, :].bitcast(I32)
+            )
+        nc.sync.dma_start(offs2_t[:], offs2)
+        load_angles(sin_t, sin_rows, 0, 0)
+        nc.sync.dma_start(wa_raw[0][:], wa_rows[:, :, :BANK])
+        load_angles(sin_t, sin_rows, 0, 1)
+        nc.sync.dma_start(wgt_t[:], wgt)
+        load_angles(cos_t, cos_rows, 0, 0)
+        load_angles(cos_t, cos_rows, 0, 1)
+        nc.sync.dma_start(wa_raw[1][:], wa_rows[:, :, BANK:])
+        for tiles, rows in ((sin_t, sin_rows), (cos_t, cos_rows)):
+            for u in range(2):
+                load_angles(tiles, rows, 1, u)
+        for b in range(2):
+            nc.sync.dma_start(wo_w[b][:].bitcast(I32), wo_words[b].rearrange("p n i -> p (n i)").bitcast(I32))
+        for q in range(4):
+            nc.sync.dma_start(
+                wo_s[32 * q : 32 * q + 4, :, :].bitcast(I32),
+                wo_scales[:, 4 * q : 4 * q + 4, :].rearrange("b r n -> r b n").bitcast(I32),
+            )
+
+        wbp_w = held("wbp_w", [P, 2 * H], U8)
+        wbp_s = held("wbp_s", [P, H], U8)
+        nc.vector.tensor_copy(
+            wbp_w[:].bitcast(U16).rearrange("k (b i p) -> k b i p", b=2, i=4),
+            wb_w[:].bitcast(U16).rearrange("k (b p i) -> k b i p", b=2, i=4),
+        )
+        v_s = held("v_s", [P, S], U8)
+        nc.vector.tensor_copy(v_s[:], tab_s[:].indirect(offs_t[:]))
+        nc.vector.tensor_copy(
+            wbp_s[:].rearrange("k (b i p) -> k b i p", b=2, i=4),
+            wb_s[:].rearrange("k (b p i) -> k b i p", b=2, i=4),
+        )
+        v_w = [held("v_w%d" % c, [P, BANK], U32) for c in range(2)]
+        for c in range(2):
+            nc.vector.tensor_copy(v_w[c][:], tab_w[:].indirect(offs_t[:, 32 * c : 32 * c + 32]))
+
+        wa_w = [held("wa_w%d" % b, [P, BANK], U32) for b in range(2)]
+        wa_s = [held("wa_s%d" % b, [P, BANK], U8) for b in range(2)]
+
+        def quantise_wa(b, copy):
+            grouped = held("wa_g%d" % b, [P, 4 * BANK], BF16)
+            copy(
+                grouped[:].rearrange("k (i p j) -> k p j i", i=4, j=4),
+                wa_raw[b][:].rearrange("k j (p i) -> k p j i", i=4),
+            )
+            nc.vector.quantize_mx(out=wa_w[b][:].bitcast(FP8X4), scales=wa_s[b][:], in_=grouped[:])
+
+        def picked(name, lhsT, lhsT_scale, angle):
+            h = hpool.tile([P, S], F32, name="h")
+            for c in range(2):
+                acc = psum.tile([P, BANK], F32, name="acc", bufs=4)
+                nc.tensor.matmul_mx(
+                    out=acc[:],
+                    lhsT=lhsT,
+                    lhsT_scale=lhsT_scale,
+                    rhs=v_w[c][:].bitcast(FP8X4),
+                    rhs_scale=v_s[:, BANK * c : BANK * (c + 1)],
+                    start=True,
+                    stop=True,
+                )
+                nc.scalar.copy(h[:, BANK * c : BANK * (c + 1)], acc[:])
+            x = held(name, [P, M], F32)
+            nc.vector.tensor_tensor(x[:], h[:].indirect(offs2_t[:]), angle, MULT)
+            return x
+
+        def sine_parts(b):
+            parts = []
+            for i in range(4):
+                c0 = P * (4 * b + i)
+                parts.append(
+                    picked(
+                        "xs%d%d" % (b, i),
+                        wbp_w[:, 2 * c0 : 2 * (c0 + P)].bitcast(FP4X4),
+                        wbp_s[:, c0 : c0 + P],
+                        sin_t[b][i // 2][:, i % 2, :],
+                    )
+                )
+            return parts
+
+        def cosine_parts(b):
+            parts = []
+            for i in range(4):
+                cols = slice(P * i, P * (i + 1))
+                parts.append(
+                    picked(
+                        "xc%d%d" % (b, i),
+                        wa_w[b][:, cols].bitcast(FP8X4),
+                        wa_s[b][:, cols],
+                        cos_t[b][i // 2][:, i % 2, :],
+                    )
+                )
+            return parts
+
+        wgt_T = held("wgt_T", [P, M], F32)
+
+        def turn_wgt():
+            bank = psum.tile([P, BANK], F32, name="back", bufs=2)
+            for c in range(4):
+                nc.tensor.transpose(bank[:, P * c : P * (c + 1)], wgt_t[:, P * c : P * (c + 1)], ident[:])
+            nc.scalar.copy(wgt_T[:], bank[:])
+
+        z_w = [[held("z_w%d%d" % (b, hf), [P, HALF], U32) for hf in range(2)] for b in range(2)]
+        z_s = [[held("z_s%d%d" % (b, hf), [P, HALF], U8) for hf in range(2)] for b in range(2)]
+
+        def join(b, hf, xc, xs, order):
+            back = psum.tile([P, BANK], F32, name="back", bufs=2)
+            for cl in range(2):
+                c = 2 * hf + cl
+                cols = slice(P * c, P * (c + 1))
+                yT = psum.tile([P, BANK], F32, name="yT", bufs=2)
+                for i in order:
+                    dst = yT[:, P * i : P * (i + 1)]
+                    nc.tensor.matmul(dst, xc[i][:, cols], ident[:], start=True, stop=False, is_transpose=True)
+                    nc.tensor.matmul(dst, xs[i][:, cols], ident[:], start=False, stop=True, is_transpose=True)
+                zT = held("zT%d%d" % (b, c), [P, BANK], BF16)
+                nc.vector.tensor_tensor(
+                    zT[:].rearrange("m (u p e) -> m u p e", u=2, e=2),
+                    yT[:].rearrange("m (u e p) -> m u p e", u=2, e=2),
+                    wgt_T[:, cols].unsqueeze(1).unsqueeze(3).to_broadcast([P, 2, P, 2]),
+                    MULT,
+                )
+                words = zT[:].bitcast(F32)
+                for u in range(2):
+                    nc.tensor.transpose(
+                        back[:, P * (2 * cl + u) : P * (2 * cl + u + 1)], words[:, P * u : P * (u + 1)], ident[:]
+                    )
+            z = held("z%d%d" % (b, hf), [P, 4 * HALF], BF16)
+            nc.scalar.copy(
+                z[:].bitcast(F32).rearrange("p (c m u) -> p c m u", c=2, u=2),
+                back[:].rearrange("p (c u m) -> p c m u", c=2, u=2),
+            )
+            nc.vector.quantize_mx(out=z_w[b][hf][:].bitcast(FP8X4), scales=z_s[b][hf][:], in_=z[:])
+
+        out_rows = out.rearrange("(c p) m -> p c m", p=P)
+
+        def project(hf):
+            for pair in range(3):
+                acc = psum.tile([P, BANK], F32, name="acc", bufs=4)
+                for cl in range(2):
+                    cols = slice(P * (2 * pair + cl), P * (2 * pair + cl + 1))
+                    for b in range(2):
+                        nc.tensor.matmul_mx(
+                            out=acc[:, HALF * cl : HALF * (cl + 1)],
+                            lhsT=wo_w[b][:, cols].bitcast(FP8X4),
+                            lhsT_scale=wo_s[:, b, cols],
+                            rhs=z_w[b][hf][:].bitcast(FP8X4),
+                            rhs_scale=z_s[b][hf][:],
+                            start=(b == 0),
+                            stop=(b == 1),
+                        )
+                res = held("res%d%d" % (hf, pair), [P, BANK], F32)
+                if (3 * hf + pair) % 2 == 0:
+                    nc.scalar.copy(res[:], acc[:])
+                else:
+                    nc.vector.tensor_copy(res[:], acc[:])
+                nc.sync.dma_start(
+                    out_rows[:, 2 * pair : 2 * pair + 2, HALF * hf : HALF * (hf + 1)],
+                    res[:].rearrange("p (c m) -> p c m", c=2),
+                )
+
+        xs0 = sine_parts(0)
+        quantise_wa(0, nc.vector.tensor_copy)
+        xc0 = cosine_parts(0)
+        turn_wgt()
+        xs1 = sine_parts(1)
+        quantise_wa(1, nc.scalar.copy)
+        for hf in range(2):
+            join(0, hf, xc0, xs0, (3, 2, 1, 0))
+        xc1 = cosine_parts(1)
+        for hf in range(2):
+            join(1, hf, xc1, xs1, (0, 1, 2, 3))
+            project(hf)

@@ -1,7 +1,6 @@
 from contextlib import ExitStack
 
 import concourse.mybir as mybir
-from concourse.masks import make_identity
 
 T, S, M, K, H, N = 4096, 1024, 512, 512, 1024, 768
 FLOPS = 2 * K * H * S * 2 + 2 * H * N * M
@@ -19,6 +18,7 @@ MULT = mybir.AluOpType.mult
 P = 128
 BANK = 512
 HALF = 256
+KB = 1024
 
 
 def tile_list_latent_key_rebuild_kernel(
@@ -27,102 +27,131 @@ def tile_list_latent_key_rebuild_kernel(
     nc = tc.nc
     with ExitStack() as ctx:
         keep = ctx.enter_context(tc.tile_pool(name="keep", bufs=1))
+        reuse = ctx.enter_context(tc.tile_pool(name="reuse", bufs=1))
         hpool = ctx.enter_context(tc.tile_pool(name="hpool", bufs=6))
         psum = ctx.enter_context(tc.psum_pool(name="psum", bufs=1))
 
-        def held(name, shape, dtype):
-            return keep.tile(shape, dtype, name=name, align_bytes=64)
+        def held(name, shape, dtype, tag=None):
+            return keep.tile(shape, dtype, name=name, tag=tag or name, align_bytes=64)
+
+        def placed(name, shape, dtype, offset):
+            return reuse.tile(shape, dtype, name=name, align_bytes=64, offset=offset)
+
+        def bank(k):
+            return psum.tile([P, BANK], F32, name="bank%d" % k)
 
         offs_t = keep.tile([P, S // 16], U16, name="offs_t")
         offs2_t = keep.tile([P, M // 16], U16, name="offs2_t")
-        tab_w = held("tab_w", [P, T], U32)
+        zeros = placed("zeros", [P, 5 * P], F32, 16 * KB - 256)
         tab_s = held("tab_s", [P, T], U8)
-        wb_w = held("wb_w", [P, 2 * H], U8)
-        wb_s = held("wb_s", [P, H], U8)
-        wo_w = [held("wo_w%d" % b, [P, N], U32) for b in range(2)]
-        wo_s = held("wo_s", [P, 2, N], U8)
-        wa_raw = [held("wa_raw%d" % b, [P, 4, BANK], F32) for b in range(2)]
-        wgt_t = held("wgt_t", [P, M], F32)
-        cos_t = [[held("cos%d%d" % (b, u), [P, 2, M], F32) for u in range(2)] for b in range(2)]
-        sin_t = [[held("sin%d%d" % (b, u), [P, 2, M], F32) for u in range(2)] for b in range(2)]
+        wb_w = placed("wb_w", [P, 2 * H], U8, 64 * KB - BANK)
         ident = held("ident", [P, P], F32)
 
         nc.vector.memset(tab_s[:].bitcast(I32), 0)
-        nc.vector.memset(wb_s[:].bitcast(I32), 0)
-        nc.vector.memset(wo_s[:].rearrange("p b n -> p (b n)").bitcast(I32), 0)
-        make_identity(nc, ident[:])
+        nc.vector.memset(zeros[:, :P], 0.0)
+        nc.gpsimd.affine_select(
+            out=ident[:],
+            in_=zeros[:, :P],
+            compare_op=mybir.AluOpType.not_equal,
+            fill=1.0,
+            base=0,
+            pattern=[[-1, P]],
+            channel_multiplier=1,
+        )
+        wb_s = [placed("wb_s0", [P, BANK], U8, 16 * KB)]
+        nc.vector.memset(wb_s[0][:].bitcast(I32), 0)
 
         tab_rows = tab_words[0].rearrange("p t i -> p (t i)").bitcast(I32)
         wa_rows = wa.rearrange("(p j) r -> p j r", j=4)
         cos_rows = cosm.rearrange("(b p i) m -> b p i m", b=2, i=4)
         sin_rows = sinm.rearrange("(b p i) m -> b p i m", b=2, i=4)
 
-        def load_angles(tiles, rows, b, u):
-            nc.sync.dma_start(tiles[b][u][:], rows[b, :, 2 * u : 2 * u + 2, :])
-
-        first = T // 4
         nc.sync.dma_start(offs_t[:], offs)
+        nc.sync.dma_start(offs2_t[:], offs2)
         nc.sync.dma_start(wb_w[:].bitcast(I32), wb_words[0].bitcast(I32))
-        nc.sync.dma_start(tab_w[:, :first].bitcast(I32), tab_rows[:, :first])
         for q in range(4):
             nc.sync.dma_start(
                 tab_s[32 * q : 32 * q + 4, :].bitcast(I32), tab_scales[0, 4 * q : 4 * q + 4, :].bitcast(I32)
             )
-        nc.sync.dma_start(tab_w[:, first:].bitcast(I32), tab_rows[:, first:])
-        for q in range(4):
-            nc.scalar.dma_start(
-                wb_s[32 * q : 32 * q + 4, :].bitcast(I32), wb_scales[0, 4 * q : 4 * q + 4, :].bitcast(I32)
-            )
-        nc.sync.dma_start(offs2_t[:], offs2)
-        load_angles(sin_t, sin_rows, 0, 0)
-        nc.sync.dma_start(wa_raw[0][:], wa_rows[:, :, :BANK])
-        load_angles(sin_t, sin_rows, 0, 1)
-        nc.sync.dma_start(wgt_t[:], wgt)
-        load_angles(cos_t, cos_rows, 0, 0)
-        load_angles(cos_t, cos_rows, 0, 1)
-        nc.sync.dma_start(wa_raw[1][:], wa_rows[:, :, BANK:])
-        for tiles, rows in ((sin_t, sin_rows), (cos_t, cos_rows)):
-            for u in range(2):
-                load_angles(tiles, rows, 1, u)
-        for b in range(2):
-            nc.sync.dma_start(wo_w[b][:].bitcast(I32), wo_words[b].rearrange("p n i -> p (n i)").bitcast(I32))
-        for q in range(4):
-            nc.sync.dma_start(
-                wo_s[32 * q : 32 * q + 4, :, :].bitcast(I32),
-                wo_scales[:, 4 * q : 4 * q + 4, :].rearrange("b r n -> r b n").bitcast(I32),
-            )
+        tab_w = placed("tab_w", [P, T], U32, 0)
+        nc.sync.dma_start(tab_w[:].bitcast(I32), tab_rows)
 
-        wbp_w = held("wbp_w", [P, 2 * H], U8)
+        def load_wb_scales(b):
+            for q in range(4):
+                nc.sync.dma_start(
+                    wb_s[b][32 * q : 32 * q + 4, :].bitcast(I32),
+                    wb_scales[0, 4 * q : 4 * q + 4, BANK * b : BANK * (b + 1)].bitcast(I32),
+                )
+
+        load_wb_scales(0)
+
+        wbp_w = placed("wbp_w", [P, 2 * H], U8, 18 * KB)
         wbp_s = held("wbp_s", [P, H], U8)
         nc.vector.tensor_copy(
             wbp_w[:].bitcast(U16).rearrange("k (b i p) -> k b i p", b=2, i=4),
             wb_w[:].bitcast(U16).rearrange("k (b p i) -> k b i p", b=2, i=4),
         )
+
+        PIECE = 1024
+        pieces = [placed("wa_first", [P, PIECE], F32, 65 * KB)[:]]
+        wb_s.append(placed("wb_s1", [P, BANK], U8, 64 * KB))
+        nc.vector.memset(wb_s[1][:].bitcast(I32), 0)
+        floats = placed("floats", [P, 11 * PIECE], F32, 20 * KB)
+        pieces.extend(floats[:, PIECE * j : PIECE * (j + 1)] for j in range(11))
+        wa_raw = [[pieces[2 * b + u].rearrange("k (j r) -> k j r", j=4) for u in range(2)] for b in range(2)]
+        sin_t = [[pieces[4 + 2 * b + u].rearrange("p (i m) -> p i m", i=2) for u in range(2)] for b in range(2)]
+        cos_t = [[pieces[8 + u].rearrange("p (i m) -> p i m", i=2) for u in range(2)]]
+        cos_late = pieces[10].rearrange("p (i m) -> p i m", i=4)
+        wgt_t = pieces[11][:, :M]
+
+        def load_angles(tiles, rows, b, u):
+            nc.sync.dma_start(tiles[b][u], rows[b, :, 2 * u : 2 * u + 2, :])
+
+        def load_wa(b):
+            for u in range(2):
+                nc.sync.dma_start(wa_raw[b][u], wa_rows[:, :, BANK * b + HALF * u : BANK * b + HALF * (u + 1)])
+
+        load_wa(0)
+        load_angles(sin_t, sin_rows, 0, 0)
+        load_wb_scales(1)
+        load_angles(sin_t, sin_rows, 0, 1)
+        nc.sync.dma_start(wgt_t, wgt)
+        load_angles(cos_t, cos_rows, 0, 0)
+        load_angles(cos_t, cos_rows, 0, 1)
+        load_angles(sin_t, sin_rows, 1, 0)
+        load_wa(1)
+        load_angles(sin_t, sin_rows, 1, 1)
+
         v_s = held("v_s", [P, S], U8)
         nc.vector.tensor_copy(v_s[:], tab_s[:].indirect(offs_t[:]))
-        nc.vector.tensor_copy(
-            wbp_s[:].rearrange("k (b i p) -> k b i p", b=2, i=4),
-            wb_s[:].rearrange("k (b p i) -> k b i p", b=2, i=4),
-        )
-        v_w = [held("v_w%d" % c, [P, BANK], U32) for c in range(2)]
-        for c in range(2):
-            nc.vector.tensor_copy(v_w[c][:], tab_w[:].indirect(offs_t[:, 32 * c : 32 * c + 32]))
+        wo_s = held("wo_s", [P, 2, N], U8, "tab_s")
+        nc.vector.memset(wo_s[:].rearrange("p b n -> p (b n)").bitcast(I32), 0)
+        v_w = [held("v_w0", [P, BANK], U32)]
+
+        def order_wb_scales(b):
+            cols = slice(BANK * b, BANK * (b + 1))
+            nc.vector.tensor_copy(
+                wbp_s[:, cols].rearrange("k (i p) -> k i p", i=4), wb_s[b][:].rearrange("k (p i) -> k i p", i=4)
+            )
 
         wa_w = [held("wa_w%d" % b, [P, BANK], U32) for b in range(2)]
         wa_s = [held("wa_s%d" % b, [P, BANK], U8) for b in range(2)]
+        wa_g = [held("wa_g%d" % b, [P, 4 * BANK], BF16) for b in range(2)]
 
-        def quantise_wa(b, copy):
-            grouped = held("wa_g%d" % b, [P, 4 * BANK], BF16)
+        def round_wa(b, u, copy):
             copy(
-                grouped[:].rearrange("k (i p j) -> k p j i", i=4, j=4),
-                wa_raw[b][:].rearrange("k j (p i) -> k p j i", i=4),
+                wa_g[b][:].rearrange("k (i p j) -> k p j i", i=4, j=4)[:, 64 * u : 64 * (u + 1)],
+                wa_raw[b][u].rearrange("k j (p i) -> k p j i", i=4),
             )
-            nc.vector.quantize_mx(out=wa_w[b][:].bitcast(FP8X4), scales=wa_s[b][:], in_=grouped[:])
 
-        def picked(name, lhsT, lhsT_scale, angle):
-            h = hpool.tile([P, S], F32, name="h")
+        def quantise_wa(b):
+            nc.vector.quantize_mx(out=wa_w[b][:].bitcast(FP8X4), scales=wa_s[b][:], in_=wa_g[b][:])
+
+        def product(lhsT, lhsT_scale, banks, h=None):
+            if h is None:
+                h = hpool.tile([P, S], F32, name="h")
             for c in range(2):
-                acc = psum.tile([P, BANK], F32, name="acc", bufs=4)
+                acc = bank(banks + c)
                 nc.tensor.matmul_mx(
                     out=acc[:],
                     lhsT=lhsT,
@@ -133,114 +162,175 @@ def tile_list_latent_key_rebuild_kernel(
                     stop=True,
                 )
                 nc.scalar.copy(h[:, BANK * c : BANK * (c + 1)], acc[:])
-            x = held(name, [P, M], F32)
-            nc.vector.tensor_tensor(x[:], h[:].indirect(offs2_t[:]), angle, MULT)
+            return h
+
+        def sine_part(b, i):
+            c0 = P * (4 * b + i)
+            h = product(wbp_w[:, 2 * c0 : 2 * (c0 + P)].bitcast(FP4X4), wbp_s[:, c0 : c0 + P], 2 * (i % 2),
+                placed("h_first%d" % i, [P, S], F32, (64 + 4 * i) * KB + BANK) if b == 0 and i < 2 else None)
+            x = held("xs%d%d" % (b, i), [P, M], F32)
+            nc.vector.tensor_tensor(x[:], h[:].indirect(offs2_t[:]), sin_t[b][i // 2][:, i % 2, :], MULT)
             return x
 
-        def sine_parts(b):
-            parts = []
-            for i in range(4):
-                c0 = P * (4 * b + i)
-                parts.append(
-                    picked(
-                        "xs%d%d" % (b, i),
-                        wbp_w[:, 2 * c0 : 2 * (c0 + P)].bitcast(FP4X4),
-                        wbp_s[:, c0 : c0 + P],
-                        sin_t[b][i // 2][:, i % 2, :],
-                    )
-                )
-            return parts
+        def cosine_product(b, i, banks):
+            cols = slice(P * i, P * (i + 1))
+            return product(wa_w[b][:, cols].bitcast(FP8X4), wa_s[b][:, cols], banks)
 
-        def cosine_parts(b):
-            parts = []
-            for i in range(4):
-                cols = slice(P * i, P * (i + 1))
-                parts.append(
-                    picked(
-                        "xc%d%d" % (b, i),
-                        wa_w[b][:, cols].bitcast(FP8X4),
-                        wa_s[b][:, cols],
-                        cos_t[b][i // 2][:, i % 2, :],
-                    )
-                )
-            return parts
+        def cosine_part(i):
+            h = cosine_product(0, i, 2 * (i % 2))
+            x = held("xc%d" % i, [P, M], F32)
+            nc.vector.tensor_tensor(x[:], h[:].indirect(offs2_t[:]), cos_t[0][i // 2][:, i % 2, :], MULT)
+            return x
 
-        wgt_T = held("wgt_T", [P, M], F32)
+        def cosine_half(h, x, i, hf):
+            nc.vector.tensor_tensor(
+                x, h[:].indirect(offs2_t[:, 16 * hf : 16 * (hf + 1)]), cos_last[hf][:, i, :], MULT
+            )
+
+        wgt_T = held("wgt_T", [P, 32], F32)
 
         def turn_wgt():
-            bank = psum.tile([P, BANK], F32, name="back", bufs=2)
+            turned = bank(4)
             for c in range(4):
-                nc.tensor.transpose(bank[:, P * c : P * (c + 1)], wgt_t[:, P * c : P * (c + 1)], ident[:])
-            nc.scalar.copy(wgt_T[:], bank[:])
+                nc.tensor.transpose(turned[:, P * c : P * (c + 1)], wgt_t[:, P * c : P * (c + 1)], ident[:])
+            nc.scalar.copy(wgt_T[:], turned[:, ::16])
 
-        z_w = [[held("z_w%d%d" % (b, hf), [P, HALF], U32) for hf in range(2)] for b in range(2)]
-        z_s = [[held("z_s%d%d" % (b, hf), [P, HALF], U8) for hf in range(2)] for b in range(2)]
+        def join(b, c, pairs, order, k):
+            cols = slice(P * c, P * (c + 1))
+            yT = bank(k)
+            for i in order:
+                dst = yT[:, P * i : P * (i + 1)]
+                one, two = pairs(i, c)
+                nc.tensor.matmul(dst, one, ident[:], start=True, stop=False, is_transpose=True)
+                nc.tensor.matmul(dst, two, ident[:], start=False, stop=True, is_transpose=True)
+            zT = held("zT%d%d" % (b, c), [P, BANK], BF16)
+            nc.vector.tensor_tensor(
+                zT[:].rearrange("m (u p e) -> m u p e", u=2, e=2),
+                yT[:].rearrange("m (u e p) -> m u p e", u=2, e=2),
+                wgt_T[:, 8 * c : 8 * (c + 1)].unsqueeze(1).unsqueeze(3).to_broadcast([P, 2, 8, 32]),
+                MULT,
+            )
+            return zT
 
-        def join(b, hf, xc, xs, order):
-            back = psum.tile([P, BANK], F32, name="back", bufs=2)
-            for cl in range(2):
-                c = 2 * hf + cl
-                cols = slice(P * c, P * (c + 1))
-                yT = psum.tile([P, BANK], F32, name="yT", bufs=2)
-                for i in order:
-                    dst = yT[:, P * i : P * (i + 1)]
-                    nc.tensor.matmul(dst, xc[i][:, cols], ident[:], start=True, stop=False, is_transpose=True)
-                    nc.tensor.matmul(dst, xs[i][:, cols], ident[:], start=False, stop=True, is_transpose=True)
-                zT = held("zT%d%d" % (b, c), [P, BANK], BF16)
-                nc.vector.tensor_tensor(
-                    zT[:].rearrange("m (u p e) -> m u p e", u=2, e=2),
-                    yT[:].rearrange("m (u e p) -> m u p e", u=2, e=2),
-                    wgt_T[:, cols].unsqueeze(1).unsqueeze(3).to_broadcast([P, 2, P, 2]),
-                    MULT,
-                )
+        def turn_back(zTs, k):
+            back = bank(k)
+            for cl, zT in enumerate(zTs):
                 words = zT[:].bitcast(F32)
                 for u in range(2):
                     nc.tensor.transpose(
                         back[:, P * (2 * cl + u) : P * (2 * cl + u + 1)], words[:, P * u : P * (u + 1)], ident[:]
                     )
-            z = held("z%d%d" % (b, hf), [P, 4 * HALF], BF16)
+            return back
+
+        def interleave_z(b, chunks, back):
+            n = len(chunks)
+            z = held("z%d%d" % (b, chunks[0]), [P, 4 * P * n], BF16)
             nc.scalar.copy(
-                z[:].bitcast(F32).rearrange("p (c m u) -> p c m u", c=2, u=2),
-                back[:].rearrange("p (c u m) -> p c m u", c=2, u=2),
+                z[:].bitcast(F32).rearrange("p (c m u) -> p c m u", c=n, u=2),
+                back[:, : 2 * P * n].rearrange("p (c u m) -> p c m u", c=n, u=2),
             )
-            nc.vector.quantize_mx(out=z_w[b][hf][:].bitcast(FP8X4), scales=z_s[b][hf][:], in_=z[:])
+            return z
+
+        def quantise(b, chunks, z, tag=None):
+            n = len(chunks)
+            name = "%d%d" % (b, chunks[0])
+            z_w = held("z_w" + name, [P, P * n], U32, tag)
+            z_s = held("z_s" + name, [P, P * n], U8)
+            nc.vector.quantize_mx(out=z_w[:].bitcast(FP8X4), scales=z_s[:], in_=z[:])
+            return z_w, z_s
+
+        def quantise_z(b, chunks, back):
+            return quantise(b, chunks, interleave_z(b, chunks, back))
 
         out_rows = out.rearrange("(c p) m -> p c m", p=P)
 
-        def project(hf):
-            for pair in range(3):
-                acc = psum.tile([P, BANK], F32, name="acc", bufs=4)
-                for cl in range(2):
-                    cols = slice(P * (2 * pair + cl), P * (2 * pair + cl + 1))
-                    for b in range(2):
-                        nc.tensor.matmul_mx(
-                            out=acc[:, HALF * cl : HALF * (cl + 1)],
-                            lhsT=wo_w[b][:, cols].bitcast(FP8X4),
-                            lhsT_scale=wo_s[:, b, cols],
-                            rhs=z_w[b][hf][:].bitcast(FP8X4),
-                            rhs_scale=z_s[b][hf][:],
-                            start=(b == 0),
-                            stop=(b == 1),
-                        )
-                res = held("res%d%d" % (hf, pair), [P, BANK], F32)
-                if (3 * hf + pair) % 2 == 0:
-                    nc.scalar.copy(res[:], acc[:])
-                else:
-                    nc.vector.tensor_copy(res[:], acc[:])
+        def project(accs, b, width, z_w, z_s):
+            per = 6 // len(accs)
+            for j, acc in enumerate(accs):
+                for cl in range(per):
+                    cols = slice(P * (per * j + cl), P * (per * j + cl + 1))
+                    nc.tensor.matmul_mx(
+                        out=acc[:, width * cl : width * (cl + 1)],
+                        lhsT=wo_w[b][:, cols].bitcast(FP8X4),
+                        lhsT_scale=wo_s[:, b, cols],
+                        rhs=z_w.bitcast(FP8X4),
+                        rhs_scale=z_s,
+                        start=(b == 0 and cl == 0),
+                        stop=(b == 1 and cl == per - 1),
+                    )
+
+        def store(accs, m0, width, copies):
+            per = 6 // len(accs)
+            for j, acc in enumerate(accs):
+                res = held("res%d_%d" % (m0, j), [P, per * width], F32)
+                copies[j](res[:], acc[:, : per * width])
                 nc.sync.dma_start(
-                    out_rows[:, 2 * pair : 2 * pair + 2, HALF * hf : HALF * (hf + 1)],
-                    res[:].rearrange("p (c m) -> p c m", c=2),
+                    out_rows[:, per * j : per * (j + 1), m0 : m0 + width], res[:].rearrange("p (c m) -> p c m", c=per)
                 )
 
-        xs0 = sine_parts(0)
-        quantise_wa(0, nc.vector.tensor_copy)
-        xc0 = cosine_parts(0)
+        nc.vector.tensor_copy(v_w[0][:], tab_w[:].indirect(offs_t[:, :32]))
+        order_wb_scales(0)
+        v_w.append(placed("v_w1", [P, BANK], U32, 16 * KB))
+        nc.vector.tensor_copy(v_w[1][:], tab_w[:].indirect(offs_t[:, 32:]))
+        cos_last = [placed("cos_last0", [P, 4, HALF], F32, 0)[:], cos_late]
+        for hf in range(2):
+            nc.sync.dma_start(cos_last[hf], cos_rows[1, :, :, HALF * hf : HALF * (hf + 1)])
+        round_wa(0, 0, nc.scalar.copy)
+        round_wa(0, 1, nc.vector.tensor_copy)
+        quantise_wa(0)
+        wo_both = held("wo_w", [P, 2 * N], U32, "wa_g0")
+        wo_w = [wo_both[:, N * b : N * (b + 1)] for b in range(2)]
+        nc.sync.dma_start(
+            wo_both[:].bitcast(I32).rearrange("p (b n) -> p b n", b=2),
+            wo_words.rearrange("b p n i -> p b (n i)").bitcast(I32),
+        )
+        for q in range(4):
+            nc.sync.dma_start(
+                wo_s[32 * q : 32 * q + 4, :, :].bitcast(I32),
+                wo_scales[:, 4 * q : 4 * q + 4, :].rearrange("b r n -> r b n").bitcast(I32),
+            )
+        xs0 = [sine_part(0, i) for i in range(4)]
+        order_wb_scales(1)
         turn_wgt()
-        xs1 = sine_parts(1)
-        quantise_wa(1, nc.scalar.copy)
-        for hf in range(2):
-            join(0, hf, xc0, xs0, (3, 2, 1, 0))
-        xc1 = cosine_parts(1)
-        for hf in range(2):
-            join(1, hf, xc1, xs1, (0, 1, 2, 3))
-            project(hf)
+        xc0 = [cosine_part(i) for i in range(4)]
+        xs1 = [sine_part(1, i) for i in range(2)]
+        for u in range(2):
+            round_wa(1, u, nc.scalar.copy)
+        quantise_wa(1)
+        def chunk(x, c):
+            return x[:, P * c : P * (c + 1)]
+
+        xs1.extend(sine_part(1, i) for i in range(2, 4))
+        zT0 = [join(0, c, lambda i, c: (chunk(xc0[i], c), chunk(xs0[i], c)), (3, 2, 1, 0), 4 + c) for c in range(4)]
+        early = held("early", [P, 4, HALF], F32)
+        hs = []
+        for i in range(4):
+            hs.append(cosine_product(1, i, 2 * i))
+            cosine_half(hs[i], early[:, i, :], i, 0)
+        backs = [turn_back(zT0[2 * hf : 2 * hf + 2], hf) for hf in range(2)]
+        z00 = quantise_z(0, (0, 1), backs[0])
+        late_a = placed("late_a", [P, 2, HALF], F32, 0)
+        for i in range(2):
+            cosine_half(hs[i], late_a[:, i, :], i, 1)
+        zT1 = [join(1, c, lambda i, c: (chunk(early[:, i, :], c), chunk(xs1[i], c)), (3, 2, 1, 0), 2 + c) for c in range(2)]
+        accs = [bank(k) for k in (4, 5, 6)]
+        project(accs, 0, HALF, z00[0][:], z00[1][:])
+        late_b = held("late_b", [P, 2, HALF], F32, "early")
+        for i in range(2):
+            cosine_half(hs[2 + i], late_b[:, i, :], 2 + i, 1)
+        late = [late_a[:, 0, :], late_a[:, 1, :], late_b[:, 0, :], late_b[:, 1, :]]
+        z01 = quantise_z(0, (2, 3), backs[1])
+        z10 = quantise_z(1, (0, 1), turn_back(zT1, 7))
+        S_, V_ = nc.scalar.copy, nc.vector.tensor_copy
+        zT1.extend(
+            join(1, c, lambda i, c: (chunk(xs1[i], c), chunk(late[i], c - 2)), (0, 1, 2, 3), c - 2) for c in (2, 3)
+        )
+        z1 = [quantise_z(1, (c,), turn_back([zT1[c]], c)) for c in (2, 3)]
+        project(accs, 1, HALF, z10[0][:], z10[1][:])
+        store(accs, 0, HALF, (S_, S_, V_))
+        tails = [[bank(k) for k in pair] for pair in ((7, 0), (1, 2))]
+        for c in (2, 3):
+            project(tails[c - 2], 0, P, chunk(z01[0], c - 2), chunk(z01[1], c - 2))
+        for c in (2, 3):
+            project(tails[c - 2], 1, P, z1[c - 2][0][:], z1[c - 2][1][:])
+            store(tails[c - 2], P * c, P, (S_, V_))

@@ -14,6 +14,7 @@ U8 = mybir.dt.uint8
 FP8X4 = mybir.dt.float8_e4m3fn_x4
 FP4X4 = mybir.dt.float4_e2m1fn_x4
 MULT = mybir.AluOpType.mult
+COPY = mybir.ActivationFunctionType.Copy
 
 P = 128
 BANK = 512
@@ -37,6 +38,9 @@ def tile_list_latent_key_rebuild_kernel(
         def placed(name, shape, dtype, offset):
             return reuse.tile(shape, dtype, name=name, align_bytes=64, offset=offset)
 
+        def chunk(x, c):
+            return x[:, P * c : P * (c + 1)]
+
         def bank(k):
             return psum.tile([P, BANK], F32, name="bank%d" % k)
 
@@ -48,7 +52,7 @@ def tile_list_latent_key_rebuild_kernel(
         ident = held("ident", [P, P], F32)
 
         nc.vector.memset(tab_s[:].bitcast(I32), 0)
-        nc.vector.memset(zeros[:, :P], 0.0)
+        nc.gpsimd.memset(zeros[:, :P], 0.0)
         nc.gpsimd.affine_select(
             out=ident[:],
             in_=zeros[:, :P],
@@ -182,10 +186,8 @@ def tile_list_latent_key_rebuild_kernel(
             nc.vector.tensor_tensor(x[:], h[:].indirect(offs2_t[:]), cos_t[0][i // 2][:, i % 2, :], MULT)
             return x
 
-        def cosine_half(h, x, i, hf):
-            nc.vector.tensor_tensor(
-                x, h[:].indirect(offs2_t[:, 16 * hf : 16 * (hf + 1)]), cos_last[hf][:, i, :], MULT
-            )
+        def cosine_piece(h, x, angle, c0, chunks):
+            nc.vector.tensor_tensor(x, h[:].indirect(offs2_t[:, 8 * c0 : 8 * (c0 + chunks)]), angle, MULT)
 
         wgt_T = held("wgt_T", [P, 32], F32)
 
@@ -195,14 +197,10 @@ def tile_list_latent_key_rebuild_kernel(
                 nc.tensor.transpose(turned[:, P * c : P * (c + 1)], wgt_t[:, P * c : P * (c + 1)], ident[:])
             nc.scalar.copy(wgt_T[:], turned[:, ::16])
 
-        def join(b, c, pairs, order, k):
-            cols = slice(P * c, P * (c + 1))
-            yT = bank(k)
-            for i in order:
-                dst = yT[:, P * i : P * (i + 1)]
-                one, two = pairs(i, c)
-                nc.tensor.matmul(dst, one, ident[:], start=True, stop=False, is_transpose=True)
-                nc.tensor.matmul(dst, two, ident[:], start=False, stop=True, is_transpose=True)
+        def add_turned(yT, i, x, first=False, last=False):
+            nc.tensor.matmul(yT[:, P * i : P * (i + 1)], x, ident[:], start=first, stop=last, is_transpose=True)
+
+        def weigh(b, c, yT):
             zT = held("zT%d%d" % (b, c), [P, BANK], BF16)
             nc.vector.tensor_tensor(
                 zT[:].rearrange("m (u p e) -> m u p e", u=2, e=2),
@@ -210,6 +208,14 @@ def tile_list_latent_key_rebuild_kernel(
                 wgt_T[:, 8 * c : 8 * (c + 1)].unsqueeze(1).unsqueeze(3).to_broadcast([P, 2, 8, 32]),
                 MULT,
             )
+            return zT
+
+        def weigh_on_scalar(b, c, yT):
+            zT = held("zT%d%d" % (b, c), [P, BANK], BF16)
+            dst = zT[:].rearrange("m (u g s e) -> m g u s e", u=2, g=8, e=2)
+            src = yT[:].rearrange("m (u e g s) -> m g u s e", u=2, e=2, g=8)
+            for g in range(8):
+                nc.scalar.activation(dst[:, g], src[:, g], COPY, scale=wgt_T[:, 8 * c + g : 8 * c + g + 1])
             return zT
 
         def turn_back(zTs, k):
@@ -222,10 +228,10 @@ def tile_list_latent_key_rebuild_kernel(
                     )
             return back
 
-        def interleave_z(b, chunks, back):
+        def interleave_z(b, chunks, back, copy=nc.scalar.copy):
             n = len(chunks)
             z = held("z%d%d" % (b, chunks[0]), [P, 4 * P * n], BF16)
-            nc.scalar.copy(
+            copy(
                 z[:].bitcast(F32).rearrange("p (c m u) -> p c m u", c=n, u=2),
                 back[:, : 2 * P * n].rearrange("p (c u m) -> p c m u", c=n, u=2),
             )
@@ -276,7 +282,10 @@ def tile_list_latent_key_rebuild_kernel(
         for hf in range(2):
             nc.sync.dma_start(cos_last[hf], cos_rows[1, :, :, HALF * hf : HALF * (hf + 1)])
         round_wa(0, 0, nc.scalar.copy)
-        round_wa(0, 1, nc.vector.tensor_copy)
+        nc.vector.tensor_copy(
+            wa_g[0][:].rearrange("k (a e p j) -> k a p j e", a=2, e=2, j=4)[:, :, 64:],
+            wa_raw[0][1].rearrange("k j (p a e) -> k a p j e", a=2, e=2),
+        )
         quantise_wa(0)
         wo_both = held("wo_w", [P, 2 * N], U32, "wa_g0")
         wo_w = [wo_both[:, N * b : N * (b + 1)] for b in range(2)]
@@ -293,44 +302,67 @@ def tile_list_latent_key_rebuild_kernel(
         order_wb_scales(1)
         turn_wgt()
         xc0 = [cosine_part(i) for i in range(4)]
-        xs1 = [sine_part(1, i) for i in range(2)]
-        for u in range(2):
-            round_wa(1, u, nc.scalar.copy)
+        xs1 = []
+        xs1.append(sine_part(1, 0))
+        xs1.append(sine_part(1, 1))
+        round_wa(1, 0, nc.scalar.copy)
+        round_wa(1, 1, nc.scalar.copy)
         quantise_wa(1)
-        def chunk(x, c):
-            return x[:, P * c : P * (c + 1)]
-
         xs1.extend(sine_part(1, i) for i in range(2, 4))
-        zT0 = [join(0, c, lambda i, c: (chunk(xc0[i], c), chunk(xs0[i], c)), (3, 2, 1, 0), 4 + c) for c in range(4)]
+        zT0 = []
+        for c in range(4):
+            yT = bank(4 + c)
+            for i in (3, 2, 1, 0):
+                add_turned(yT, i, chunk(xc0[i], c), first=True)
+                add_turned(yT, i, chunk(xs0[i], c), last=True)
+            zT0.append(weigh(0, c, yT))
         early = held("early", [P, 4, HALF], F32)
         hs = []
         for i in range(4):
             hs.append(cosine_product(1, i, 2 * i))
-            cosine_half(hs[i], early[:, i, :], i, 0)
+            cosine_piece(hs[i], early[:, i, :], cos_last[0][:, i, :], 0, 2)
         backs = [turn_back(zT0[2 * hf : 2 * hf + 2], hf) for hf in range(2)]
         z00 = quantise_z(0, (0, 1), backs[0])
-        late_a = placed("late_a", [P, 2, HALF], F32, 0)
-        for i in range(2):
-            cosine_half(hs[i], late_a[:, i, :], i, 1)
-        zT1 = [join(1, c, lambda i, c: (chunk(early[:, i, :], c), chunk(xs1[i], c)), (3, 2, 1, 0), 2 + c) for c in range(2)]
-        accs = [bank(k) for k in (4, 5, 6)]
-        project(accs, 0, HALF, z00[0][:], z00[1][:])
-        late_b = held("late_b", [P, 2, HALF], F32, "early")
-        for i in range(2):
-            cosine_half(hs[2 + i], late_b[:, i, :], 2 + i, 1)
-        late = [late_a[:, 0, :], late_a[:, 1, :], late_b[:, 0, :], late_b[:, 1, :]]
-        z01 = quantise_z(0, (2, 3), backs[1])
-        z10 = quantise_z(1, (0, 1), turn_back(zT1, 7))
+        z01_bf = interleave_z(0, (2, 3), backs[1])
         S_, V_ = nc.scalar.copy, nc.vector.tensor_copy
-        zT1.extend(
-            join(1, c, lambda i, c: (chunk(xs1[i], c), chunk(late[i], c - 2)), (0, 1, 2, 3), c - 2) for c in (2, 3)
-        )
-        z1 = [quantise_z(1, (c,), turn_back([zT1[c]], c)) for c in (2, 3)]
-        project(accs, 1, HALF, z10[0][:], z10[1][:])
-        store(accs, 0, HALF, (S_, S_, V_))
-        tails = [[bank(k) for k in pair] for pair in ((7, 0), (1, 2))]
+
+        yT1 = [bank(k) for k in (2, 3, 0, 1)]
+        zT1 = []
+        for c in range(2):
+            for i in range(4):
+                add_turned(yT1[c], i, chunk(xs1[i], c), first=(i == 0))
+        for i in range(4):
+            for c in range(2):
+                add_turned(yT1[c], i, chunk(early[:, i, :], c), last=(i == 3))
+        zT1.extend(weigh_on_scalar(1, c, yT1[c]) for c in range(2))
+        back_a = turn_back(zT1, 7)
         for c in (2, 3):
-            project(tails[c - 2], 0, P, chunk(z01[0], c - 2), chunk(z01[1], c - 2))
-        for c in (2, 3):
-            project(tails[c - 2], 1, P, z1[c - 2][0][:], z1[c - 2][1][:])
-            store(tails[c - 2], P * c, P, (S_, V_))
+            for i in range(4):
+                add_turned(yT1[c], i, chunk(xs1[i], c), first=(i == 0))
+        late_b = placed("late_b", [P, 4, P], F32, 0)
+        for i in range(4):
+            cosine_piece(hs[i], late_b[:, i, :], cos_last[1][:, i, :P], 2, 1)
+            add_turned(yT1[2], i, late_b[:, i, :], last=(i == 3))
+        out_a = [bank(k) for k in (4, 5, 6)]
+        project(out_a, 0, HALF, z00[0][:], z00[1][:])
+        za_bf = interleave_z(1, (0, 1), back_a)
+        zb_bf = interleave_z(1, (2,), turn_back([weigh(1, 2, yT1[2])], 2), S_)
+        z01 = quantise(0, (2, 3), z01_bf)
+        out_b = [bank(k) for k in (7, 0)]
+        project(out_b, 0, P, chunk(z01[0], 0), chunk(z01[1], 0))
+        za = quantise(1, (0, 1), za_bf)
+        zb = quantise(1, (2,), zb_bf)
+        project(out_a, 1, HALF, za[0][:], za[1][:])
+        project(out_b, 1, P, zb[0][:], zb[1][:])
+        late_c = [placed("late_c0", [P, 2, P], F32, 0), held("late_c1", [P, 2, P], F32, "z12")]
+        for i in range(4):
+            x = late_c[i // 2][:, i % 2, :]
+            cosine_piece(hs[i], x, cos_last[1][:, i, P:], 3, 1)
+            add_turned(yT1[3], i, x, last=(i == 3))
+        zc = quantise(1, (3,), interleave_z(1, (3,), turn_back([weigh(1, 3, yT1[3])], 3), V_))
+        store(out_a, 0, HALF, (S_, S_, S_))
+        store(out_b, 2 * P, P, (S_, S_))
+        out_c = [bank(k) for k in (2, 4)]
+        project(out_c, 0, P, chunk(z01[0], 1), chunk(z01[1], 1))
+        project(out_c, 1, P, zc[0][:], zc[1][:])
+        store(out_c, 3 * P, P, (S_, V_))

@@ -19,7 +19,21 @@ COPY = mybir.ActivationFunctionType.Copy
 P = 128
 BANK = 512
 HALF = 256
+PIECE = 1024
+GROUPS = 8
+H_TILES = 6
 KB = 1024
+
+AT_TABLE = 0
+AT_WB_SCALES_0 = 16 * KB
+AT_WB_ORDERED = 18 * KB
+AT_ZEROS = AT_WB_SCALES_0 - 256
+ZEROS_COLUMNS = 5 * P
+AT_FLOATS = 20 * KB
+AT_WB_SCALES_1 = 64 * KB
+AT_WA_FIRST = 65 * KB
+AT_WB_WORDS = AT_WB_SCALES_1 - 512
+AT_H_FIRST = AT_WB_SCALES_1 + 512
 
 
 def tile_list_latent_key_rebuild_kernel(
@@ -29,7 +43,7 @@ def tile_list_latent_key_rebuild_kernel(
     with ExitStack() as ctx:
         keep = ctx.enter_context(tc.tile_pool(name="keep", bufs=1))
         reuse = ctx.enter_context(tc.tile_pool(name="reuse", bufs=1))
-        hpool = ctx.enter_context(tc.tile_pool(name="hpool", bufs=6))
+        ring = ctx.enter_context(tc.tile_pool(name="ring", bufs=H_TILES))
         psum = ctx.enter_context(tc.psum_pool(name="psum", bufs=1))
 
         def held(name, shape, dtype, tag=None):
@@ -44,11 +58,16 @@ def tile_list_latent_key_rebuild_kernel(
         def bank(k):
             return psum.tile([P, BANK], F32, name="bank%d" % k)
 
+        def scale_rows(plane, q):
+            return plane[32 * q : 32 * q + 4]
+
+        on_scalar, on_vector = nc.scalar.copy, nc.vector.tensor_copy
+
         offs_t = keep.tile([P, S // 16], U16, name="offs_t")
         offs2_t = keep.tile([P, M // 16], U16, name="offs2_t")
-        zeros = placed("zeros", [P, 5 * P], F32, 16 * KB - 256)
+        zeros = placed("zeros", [P, ZEROS_COLUMNS], F32, AT_ZEROS)
         tab_s = held("tab_s", [P, T], U8)
-        wb_w = placed("wb_w", [P, 2 * H], U8, 64 * KB - BANK)
+        wb_w = placed("wb_w", [P, 2 * H], U8, AT_WB_WORDS)
         ident = held("ident", [P, P], F32)
 
         nc.vector.memset(tab_s[:].bitcast(I32), 0)
@@ -62,7 +81,7 @@ def tile_list_latent_key_rebuild_kernel(
             pattern=[[-1, P]],
             channel_multiplier=1,
         )
-        wb_s = [placed("wb_s0", [P, BANK], U8, 16 * KB)]
+        wb_s = [placed("wb_s0", [P, BANK], U8, AT_WB_SCALES_0)]
         nc.vector.memset(wb_s[0][:].bitcast(I32), 0)
 
         tab_rows = tab_words[0].rearrange("p t i -> p (t i)").bitcast(I32)
@@ -74,57 +93,54 @@ def tile_list_latent_key_rebuild_kernel(
         nc.sync.dma_start(offs2_t[:], offs2)
         nc.sync.dma_start(wb_w[:].bitcast(I32), wb_words[0].bitcast(I32))
         for q in range(4):
-            nc.sync.dma_start(
-                tab_s[32 * q : 32 * q + 4, :].bitcast(I32), tab_scales[0, 4 * q : 4 * q + 4, :].bitcast(I32)
-            )
-        tab_w = placed("tab_w", [P, T], U32, 0)
+            nc.sync.dma_start(scale_rows(tab_s, q).bitcast(I32), tab_scales[0, 4 * q : 4 * q + 4, :].bitcast(I32))
+        tab_w = placed("tab_w", [P, T], U32, AT_TABLE)
         nc.sync.dma_start(tab_w[:].bitcast(I32), tab_rows)
 
         def load_wb_scales(b):
             for q in range(4):
                 nc.sync.dma_start(
-                    wb_s[b][32 * q : 32 * q + 4, :].bitcast(I32),
+                    scale_rows(wb_s[b], q).bitcast(I32),
                     wb_scales[0, 4 * q : 4 * q + 4, BANK * b : BANK * (b + 1)].bitcast(I32),
                 )
 
         load_wb_scales(0)
 
-        wbp_w = placed("wbp_w", [P, 2 * H], U8, 18 * KB)
+        wbp_w = placed("wbp_w", [P, 2 * H], U8, AT_WB_ORDERED)
         wbp_s = held("wbp_s", [P, H], U8)
         nc.vector.tensor_copy(
             wbp_w[:].bitcast(U16).rearrange("k (b i p) -> k b i p", b=2, i=4),
             wb_w[:].bitcast(U16).rearrange("k (b p i) -> k b i p", b=2, i=4),
         )
 
-        PIECE = 1024
-        pieces = [placed("wa_first", [P, PIECE], F32, 65 * KB)[:]]
-        wb_s.append(placed("wb_s1", [P, BANK], U8, 64 * KB))
+        pieces = [placed("wa_first", [P, PIECE], F32, AT_WA_FIRST)[:]]
+        wb_s.append(placed("wb_s1", [P, BANK], U8, AT_WB_SCALES_1))
         nc.vector.memset(wb_s[1][:].bitcast(I32), 0)
-        floats = placed("floats", [P, 11 * PIECE], F32, 20 * KB)
+        floats = placed("floats", [P, 11 * PIECE], F32, AT_FLOATS)
         pieces.extend(floats[:, PIECE * j : PIECE * (j + 1)] for j in range(11))
         wa_raw = [[pieces[2 * b + u].rearrange("k (j r) -> k j r", j=4) for u in range(2)] for b in range(2)]
         sin_t = [[pieces[4 + 2 * b + u].rearrange("p (i m) -> p i m", i=2) for u in range(2)] for b in range(2)]
-        cos_t = [[pieces[8 + u].rearrange("p (i m) -> p i m", i=2) for u in range(2)]]
-        cos_late = pieces[10].rearrange("p (i m) -> p i m", i=4)
+        cos_0 = [pieces[8 + u].rearrange("p (i m) -> p i m", i=2) for u in range(2)]
+        cos_1_late = pieces[10].rearrange("p (i m) -> p i m", i=4)
         wgt_t = pieces[11][:, :M]
 
-        def load_angles(tiles, rows, b, u):
-            nc.sync.dma_start(tiles[b][u], rows[b, :, 2 * u : 2 * u + 2, :])
+        def load_planes(tiles, rows, u):
+            nc.sync.dma_start(tiles[u], rows[:, 2 * u : 2 * u + 2, :])
 
         def load_wa(b):
             for u in range(2):
                 nc.sync.dma_start(wa_raw[b][u], wa_rows[:, :, BANK * b + HALF * u : BANK * b + HALF * (u + 1)])
 
         load_wa(0)
-        load_angles(sin_t, sin_rows, 0, 0)
+        load_planes(sin_t[0], sin_rows[0], 0)
         load_wb_scales(1)
-        load_angles(sin_t, sin_rows, 0, 1)
+        load_planes(sin_t[0], sin_rows[0], 1)
         nc.sync.dma_start(wgt_t, wgt)
-        load_angles(cos_t, cos_rows, 0, 0)
-        load_angles(cos_t, cos_rows, 0, 1)
-        load_angles(sin_t, sin_rows, 1, 0)
+        load_planes(cos_0, cos_rows[0], 0)
+        load_planes(cos_0, cos_rows[0], 1)
+        load_planes(sin_t[1], sin_rows[1], 0)
         load_wa(1)
-        load_angles(sin_t, sin_rows, 1, 1)
+        load_planes(sin_t[1], sin_rows[1], 1)
 
         v_s = held("v_s", [P, S], U8)
         nc.vector.tensor_copy(v_s[:], tab_s[:].indirect(offs_t[:]))
@@ -133,29 +149,27 @@ def tile_list_latent_key_rebuild_kernel(
         v_w = [held("v_w0", [P, BANK], U32)]
 
         def order_wb_scales(b):
-            cols = slice(BANK * b, BANK * (b + 1))
             nc.vector.tensor_copy(
-                wbp_s[:, cols].rearrange("k (i p) -> k i p", i=4), wb_s[b][:].rearrange("k (p i) -> k i p", i=4)
+                wbp_s[:, BANK * b : BANK * (b + 1)].rearrange("k (i p) -> k i p", i=4),
+                wb_s[b][:].rearrange("k (p i) -> k i p", i=4),
             )
 
         wa_w = [held("wa_w%d" % b, [P, BANK], U32) for b in range(2)]
         wa_s = [held("wa_s%d" % b, [P, BANK], U8) for b in range(2)]
-        wa_g = [held("wa_g%d" % b, [P, 4 * BANK], BF16) for b in range(2)]
+        wa_bf = [held("wa_bf%d" % b, [P, 4 * BANK], BF16) for b in range(2)]
 
-        def round_wa(b, u, copy):
-            copy(
-                wa_g[b][:].rearrange("k (i p j) -> k p j i", i=4, j=4)[:, 64 * u : 64 * (u + 1)],
+        def round_wa_on_scalar(b, u):
+            nc.scalar.copy(
+                wa_bf[b][:].rearrange("k (i p j) -> k p j i", i=4, j=4)[:, 64 * u : 64 * (u + 1)],
                 wa_raw[b][u].rearrange("k j (p i) -> k p j i", i=4),
             )
 
         def quantise_wa(b):
-            nc.vector.quantize_mx(out=wa_w[b][:].bitcast(FP8X4), scales=wa_s[b][:], in_=wa_g[b][:])
+            nc.vector.quantize_mx(out=wa_w[b][:].bitcast(FP8X4), scales=wa_s[b][:], in_=wa_bf[b][:])
 
-        def product(lhsT, lhsT_scale, banks, h=None):
-            if h is None:
-                h = hpool.tile([P, S], F32, name="h")
+        def product(lhsT, lhsT_scale, first_bank, h):
             for c in range(2):
-                acc = bank(banks + c)
+                acc = bank(first_bank + c)
                 nc.tensor.matmul_mx(
                     out=acc[:],
                     lhsT=lhsT,
@@ -168,105 +182,101 @@ def tile_list_latent_key_rebuild_kernel(
                 nc.scalar.copy(h[:, BANK * c : BANK * (c + 1)], acc[:])
             return h
 
-        def sine_part(b, i):
+        def next_h():
+            return ring.tile([P, S], F32, name="h")
+
+        def pick(x, h, angle, first_chunk, chunks):
+            offsets = offs2_t[:, 8 * first_chunk : 8 * (first_chunk + chunks)]
+            nc.vector.tensor_tensor(x, h[:].indirect(offsets), angle, MULT)
+
+        def sine_part(b, i, h):
             c0 = P * (4 * b + i)
-            h = product(wbp_w[:, 2 * c0 : 2 * (c0 + P)].bitcast(FP4X4), wbp_s[:, c0 : c0 + P], 2 * (i % 2),
-                placed("h_first%d" % i, [P, S], F32, (64 + 4 * i) * KB + BANK) if b == 0 and i < 2 else None)
+            product(wbp_w[:, 2 * c0 : 2 * (c0 + P)].bitcast(FP4X4), wbp_s[:, c0 : c0 + P], 2 * (i % 2), h)
             x = held("xs%d%d" % (b, i), [P, M], F32)
-            nc.vector.tensor_tensor(x[:], h[:].indirect(offs2_t[:]), sin_t[b][i // 2][:, i % 2, :], MULT)
+            pick(x[:], h, sin_t[b][i // 2][:, i % 2, :], 0, 4)
             return x
 
-        def cosine_product(b, i, banks):
-            cols = slice(P * i, P * (i + 1))
-            return product(wa_w[b][:, cols].bitcast(FP8X4), wa_s[b][:, cols], banks)
+        def cosine_product(b, i, first_bank):
+            return product(chunk(wa_w[b], i).bitcast(FP8X4), chunk(wa_s[b], i), first_bank, next_h())
 
-        def cosine_part(i):
+        def cosine_part_0(i):
             h = cosine_product(0, i, 2 * (i % 2))
             x = held("xc%d" % i, [P, M], F32)
-            nc.vector.tensor_tensor(x[:], h[:].indirect(offs2_t[:]), cos_t[0][i // 2][:, i % 2, :], MULT)
+            pick(x[:], h, cos_0[i // 2][:, i % 2, :], 0, 4)
             return x
 
-        def cosine_piece(h, x, angle, c0, chunks):
-            nc.vector.tensor_tensor(x, h[:].indirect(offs2_t[:, 8 * c0 : 8 * (c0 + chunks)]), angle, MULT)
-
-        wgt_T = held("wgt_T", [P, 32], F32)
+        wgt_T = held("wgt_T", [P, 4 * GROUPS], F32)
 
         def turn_wgt():
             turned = bank(4)
             for c in range(4):
-                nc.tensor.transpose(turned[:, P * c : P * (c + 1)], wgt_t[:, P * c : P * (c + 1)], ident[:])
+                nc.tensor.transpose(chunk(turned, c), chunk(wgt_t, c), ident[:])
             nc.scalar.copy(wgt_T[:], turned[:, ::16])
 
-        def add_turned(yT, i, x, first=False, last=False):
-            nc.tensor.matmul(yT[:, P * i : P * (i + 1)], x, ident[:], start=first, stop=last, is_transpose=True)
+        def add_turned(y, i, x, first=False, last=False):
+            nc.tensor.matmul(chunk(y, i), x, ident[:], start=first, stop=last, is_transpose=True)
 
-        def weigh(b, c, yT):
+        def weigh_on_vector(b, c, y):
             zT = held("zT%d%d" % (b, c), [P, BANK], BF16)
             nc.vector.tensor_tensor(
                 zT[:].rearrange("m (u p e) -> m u p e", u=2, e=2),
-                yT[:].rearrange("m (u e p) -> m u p e", u=2, e=2),
-                wgt_T[:, 8 * c : 8 * (c + 1)].unsqueeze(1).unsqueeze(3).to_broadcast([P, 2, 8, 32]),
+                y[:].rearrange("m (u e p) -> m u p e", u=2, e=2),
+                wgt_T[:, GROUPS * c : GROUPS * (c + 1)].unsqueeze(1).unsqueeze(3).to_broadcast([P, 2, GROUPS, 32]),
                 MULT,
             )
             return zT
 
-        def weigh_on_scalar(b, c, yT):
+        def weigh_on_scalar(b, c, y):
             zT = held("zT%d%d" % (b, c), [P, BANK], BF16)
-            dst = zT[:].rearrange("m (u g s e) -> m g u s e", u=2, g=8, e=2)
-            src = yT[:].rearrange("m (u e g s) -> m g u s e", u=2, e=2, g=8)
-            for g in range(8):
-                nc.scalar.activation(dst[:, g], src[:, g], COPY, scale=wgt_T[:, 8 * c + g : 8 * c + g + 1])
+            dst = zT[:].rearrange("m (u g s e) -> m g u s e", u=2, g=GROUPS, e=2)
+            src = y[:].rearrange("m (u e g s) -> m g u s e", u=2, e=2, g=GROUPS)
+            for g in range(GROUPS):
+                column = GROUPS * c + g
+                nc.scalar.activation(dst[:, g], src[:, g], COPY, scale=wgt_T[:, column : column + 1])
             return zT
+
+        def turn_words(back, slot, zT):
+            words = zT[:].bitcast(F32)
+            for u in range(2):
+                nc.tensor.transpose(chunk(back, 2 * slot + u), chunk(words, u), ident[:])
 
         def turn_back(zTs, k):
             back = bank(k)
-            for cl, zT in enumerate(zTs):
-                words = zT[:].bitcast(F32)
-                for u in range(2):
-                    nc.tensor.transpose(
-                        back[:, P * (2 * cl + u) : P * (2 * cl + u + 1)], words[:, P * u : P * (u + 1)], ident[:]
-                    )
+            for slot, zT in enumerate(zTs):
+                turn_words(back, slot, zT)
             return back
 
-        def interleave_z(b, chunks, back, copy=nc.scalar.copy):
-            n = len(chunks)
-            z = held("z%d%d" % (b, chunks[0]), [P, 4 * P * n], BF16)
+        def interleave_z(name, chunks, back, copy):
+            z = held("z" + name, [P, 4 * P * chunks], BF16)
             copy(
-                z[:].bitcast(F32).rearrange("p (c m u) -> p c m u", c=n, u=2),
-                back[:, : 2 * P * n].rearrange("p (c u m) -> p c m u", c=n, u=2),
+                z[:].bitcast(F32).rearrange("p (c m u) -> p c m u", c=chunks, u=2),
+                back[:, : 2 * P * chunks].rearrange("p (c u m) -> p c m u", c=chunks, u=2),
             )
             return z
 
-        def quantise(b, chunks, z, tag=None):
-            n = len(chunks)
-            name = "%d%d" % (b, chunks[0])
-            z_w = held("z_w" + name, [P, P * n], U32, tag)
-            z_s = held("z_s" + name, [P, P * n], U8)
+        def quantise_z(name, chunks, z):
+            z_w = held("z_w" + name, [P, P * chunks], U32)
+            z_s = held("z_s" + name, [P, P * chunks], U8)
             nc.vector.quantize_mx(out=z_w[:].bitcast(FP8X4), scales=z_s[:], in_=z[:])
-            return z_w, z_s
-
-        def quantise_z(b, chunks, back):
-            return quantise(b, chunks, interleave_z(b, chunks, back))
+            return z_w[:], z_s[:]
 
         out_rows = out.rearrange("(c p) m -> p c m", p=P)
 
-        def project(accs, b, width, z_w, z_s):
-            per = 6 // len(accs)
-            for j, acc in enumerate(accs):
-                for cl in range(per):
-                    cols = slice(P * (per * j + cl), P * (per * j + cl + 1))
-                    nc.tensor.matmul_mx(
-                        out=acc[:, width * cl : width * (cl + 1)],
-                        lhsT=wo_w[b][:, cols].bitcast(FP8X4),
-                        lhsT_scale=wo_s[:, b, cols],
-                        rhs=z_w.bitcast(FP8X4),
-                        rhs_scale=z_s,
-                        start=(b == 0 and cl == 0),
-                        stop=(b == 1 and cl == per - 1),
-                    )
+        def project(acc, row_tiles, b, z_w, z_s):
+            width = z_w.shape[1]
+            for slot, n in enumerate(row_tiles):
+                nc.tensor.matmul_mx(
+                    out=acc[:, width * slot : width * (slot + 1)],
+                    lhsT=chunk(wo_w[b], n).bitcast(FP8X4),
+                    lhsT_scale=chunk(wo_s[:, b, :], n),
+                    rhs=z_w.bitcast(FP8X4),
+                    rhs_scale=z_s,
+                    start=(b == 0 and slot == 0),
+                    stop=(b == 1 and slot == len(row_tiles) - 1),
+                )
 
         def store(accs, m0, width, copies):
-            per = 6 // len(accs)
+            per = N // P // len(accs)
             for j, acc in enumerate(accs):
                 res = held("res%d_%d" % (m0, j), [P, per * width], F32)
                 copies[j](res[:], acc[:, : per * width])
@@ -276,18 +286,18 @@ def tile_list_latent_key_rebuild_kernel(
 
         nc.vector.tensor_copy(v_w[0][:], tab_w[:].indirect(offs_t[:, :32]))
         order_wb_scales(0)
-        v_w.append(placed("v_w1", [P, BANK], U32, 16 * KB))
+        v_w.append(placed("v_w1", [P, BANK], U32, AT_WB_SCALES_0))
         nc.vector.tensor_copy(v_w[1][:], tab_w[:].indirect(offs_t[:, 32:]))
-        cos_last = [placed("cos_last0", [P, 4, HALF], F32, 0)[:], cos_late]
-        for hf in range(2):
-            nc.sync.dma_start(cos_last[hf], cos_rows[1, :, :, HALF * hf : HALF * (hf + 1)])
-        round_wa(0, 0, nc.scalar.copy)
+        cos_1_early = placed("cos_1_early", [P, 4, HALF], F32, AT_TABLE)
+        nc.sync.dma_start(cos_1_early[:], cos_rows[1, :, :, :HALF])
+        nc.sync.dma_start(cos_1_late, cos_rows[1, :, :, HALF:])
+        round_wa_on_scalar(0, 0)
         nc.vector.tensor_copy(
-            wa_g[0][:].rearrange("k (a e p j) -> k a p j e", a=2, e=2, j=4)[:, :, 64:],
+            wa_bf[0][:].rearrange("k (a e p j) -> k a p j e", a=2, e=2, j=4)[:, :, 64:],
             wa_raw[0][1].rearrange("k j (p a e) -> k a p j e", a=2, e=2),
         )
         quantise_wa(0)
-        wo_both = held("wo_w", [P, 2 * N], U32, "wa_g0")
+        wo_both = held("wo_w", [P, 2 * N], U32, "wa_bf0")
         wo_w = [wo_both[:, N * b : N * (b + 1)] for b in range(2)]
         nc.sync.dma_start(
             wo_both[:].bitcast(I32).rearrange("p (b n) -> p b n", b=2),
@@ -295,74 +305,104 @@ def tile_list_latent_key_rebuild_kernel(
         )
         for q in range(4):
             nc.sync.dma_start(
-                wo_s[32 * q : 32 * q + 4, :, :].bitcast(I32),
+                scale_rows(wo_s, q).bitcast(I32),
                 wo_scales[:, 4 * q : 4 * q + 4, :].rearrange("b r n -> r b n").bitcast(I32),
             )
-        xs0 = [sine_part(0, i) for i in range(4)]
+
+        xs0 = [sine_part(0, i, placed("h_first%d" % i, [P, S], F32, AT_H_FIRST + 4 * KB * i)) for i in range(2)]
+        xs0.extend(sine_part(0, i, next_h()) for i in range(2, 4))
         order_wb_scales(1)
         turn_wgt()
-        xc0 = [cosine_part(i) for i in range(4)]
-        xs1 = []
-        xs1.append(sine_part(1, 0))
-        xs1.append(sine_part(1, 1))
-        round_wa(1, 0, nc.scalar.copy)
-        round_wa(1, 1, nc.scalar.copy)
-        quantise_wa(1)
-        xs1.extend(sine_part(1, i) for i in range(2, 4))
-        zT0 = []
-        for c in range(4):
-            yT = bank(4 + c)
-            for i in (3, 2, 1, 0):
-                add_turned(yT, i, chunk(xc0[i], c), first=True)
-                add_turned(yT, i, chunk(xs0[i], c), last=True)
-            zT0.append(weigh(0, c, yT))
-        early = held("early", [P, 4, HALF], F32)
-        hs = []
-        for i in range(4):
-            hs.append(cosine_product(1, i, 2 * i))
-            cosine_piece(hs[i], early[:, i, :], cos_last[0][:, i, :], 0, 2)
-        backs = [turn_back(zT0[2 * hf : 2 * hf + 2], hf) for hf in range(2)]
-        z00 = quantise_z(0, (0, 1), backs[0])
-        z01_bf = interleave_z(0, (2, 3), backs[1])
-        S_, V_ = nc.scalar.copy, nc.vector.tensor_copy
+        xc0 = [cosine_part_0(i) for i in range(4)]
 
-        yT1 = [bank(k) for k in (2, 3, 0, 1)]
-        zT1 = []
-        for c in range(2):
+        xs1 = [sine_part(1, i, next_h()) for i in range(2)]
+        for u in range(2):
+            round_wa_on_scalar(1, u)
+        quantise_wa(1)
+
+        def join_0(c):
+            y = bank(4 + c)
+            for i in reversed(range(4)):
+                add_turned(y, i, chunk(xc0[i], c), first=True)
+                add_turned(y, i, chunk(xs0[i], c), last=True)
+            return weigh_on_vector(0, c, y)
+
+        early = held("early", [P, 4, HALF], F32)
+        ha1 = []
+
+        def early_part(i, first_bank):
+            ha1.append(cosine_product(1, i, first_bank))
+            pick(early[:, i, :], ha1[i], cos_1_early[:, i, :], 0, 2)
+
+        zT0 = [join_0(0)]
+        xs1.extend(sine_part(1, i, next_h()) for i in range(2, 4))
+        zT0.append(join_0(1))
+        early_part(0, 0)
+        zT0.append(join_0(2))
+        early_part(1, 2)
+        zT0.append(join_0(3))
+        early_part(2, 4)
+        early_part(3, 0)
+
+        def open_sum(c, k):
+            y = bank(k)
             for i in range(4):
-                add_turned(yT1[c], i, chunk(xs1[i], c), first=(i == 0))
+                add_turned(y, i, chunk(xs1[i], c), first=(i == 0))
+            return y
+
+        def add_early(planes):
+            for i in planes:
+                for c in range(2):
+                    add_turned(y1[c], i, chunk(early[:, i, :], c), last=(i == 3))
+
+        z0_a = quantise_z("0a", 2, interleave_z("0a", 2, turn_back(zT0[:2], 6), on_scalar))
+        y1 = [open_sum(c, 2 + c) for c in range(2)]
+        add_early(range(2))
+        z0_bc_bf = interleave_z("0bc", 2, turn_back(zT0[2:], 7), on_scalar)
+        add_early(range(2, 4))
+        zT1 = [weigh_on_scalar(1, c, y1[c]) for c in range(2)]
+        y1.extend(open_sum(c, 4 + c) for c in range(2, 4))
+        back_a = bank(1)
+        turn_words(back_a, 0, zT1[0])
+        late_b = placed("late_b", [P, 4, P], F32, AT_TABLE)
         for i in range(4):
-            for c in range(2):
-                add_turned(yT1[c], i, chunk(early[:, i, :], c), last=(i == 3))
-        zT1.extend(weigh_on_scalar(1, c, yT1[c]) for c in range(2))
-        back_a = turn_back(zT1, 7)
-        for c in (2, 3):
-            for i in range(4):
-                add_turned(yT1[c], i, chunk(xs1[i], c), first=(i == 0))
-        late_b = placed("late_b", [P, 4, P], F32, 0)
+            pick(late_b[:, i, :], ha1[i], cos_1_late[:, i, :P], 2, 1)
+            add_turned(y1[2], i, late_b[:, i, :], last=(i == 3))
+        z0_bc = quantise_z("0bc", 2, z0_bc_bf)
+        z0_b, z0_c = [(chunk(z0_bc[0], c), chunk(z0_bc[1], c)) for c in range(2)]
+        zT1.append(weigh_on_vector(1, 2, y1[2]))
+
+        pairs = [range(2 * j, 2 * j + 2) for j in range(3)]
+        triples = [range(3 * j, 3 * j + 3) for j in range(2)]
+        out_a = [bank(k) for k in (4, 5, 0)]
+        for j in range(2):
+            project(out_a[j], pairs[j], 0, *z0_a)
+        turn_words(back_a, 1, zT1[1])
+        back_b = turn_back(zT1[2:], 2)
+        project(out_a[2], pairs[2], 0, *z0_a)
+        z1_a_bf = interleave_z("1a", 2, back_a, on_scalar)
+        z1_b_bf = interleave_z("1b", 1, back_b, on_scalar)
+        out_b = [bank(k) for k in (6, 1)]
+        for j in range(2):
+            project(out_b[j], triples[j], 0, *z0_b)
+        late_c = placed("late_c", [P, 4, P], F32, AT_TABLE)
         for i in range(4):
-            cosine_piece(hs[i], late_b[:, i, :], cos_last[1][:, i, :P], 2, 1)
-            add_turned(yT1[2], i, late_b[:, i, :], last=(i == 3))
-        out_a = [bank(k) for k in (4, 5, 6)]
-        project(out_a, 0, HALF, z00[0][:], z00[1][:])
-        za_bf = interleave_z(1, (0, 1), back_a)
-        zb_bf = interleave_z(1, (2,), turn_back([weigh(1, 2, yT1[2])], 2), S_)
-        z01 = quantise(0, (2, 3), z01_bf)
-        out_b = [bank(k) for k in (7, 0)]
-        project(out_b, 0, P, chunk(z01[0], 0), chunk(z01[1], 0))
-        za = quantise(1, (0, 1), za_bf)
-        zb = quantise(1, (2,), zb_bf)
-        project(out_a, 1, HALF, za[0][:], za[1][:])
-        project(out_b, 1, P, zb[0][:], zb[1][:])
-        late_c = [placed("late_c0", [P, 2, P], F32, 0), held("late_c1", [P, 2, P], F32, "z12")]
+            pick(late_c[:, i, :], ha1[i], cos_1_late[:, i, P:], 3, 1)
+        z1_a = quantise_z("1a", 2, z1_a_bf)
+        z1_b = quantise_z("1b", 1, z1_b_bf)
         for i in range(4):
-            x = late_c[i // 2][:, i % 2, :]
-            cosine_piece(hs[i], x, cos_last[1][:, i, P:], 3, 1)
-            add_turned(yT1[3], i, x, last=(i == 3))
-        zc = quantise(1, (3,), interleave_z(1, (3,), turn_back([weigh(1, 3, yT1[3])], 3), V_))
-        store(out_a, 0, HALF, (S_, S_, S_))
-        store(out_b, 2 * P, P, (S_, S_))
+            add_turned(y1[3], i, late_c[:, i, :], last=(i == 3))
+        zT1.append(weigh_on_vector(1, 3, y1[3]))
+        z1_c = quantise_z("1c", 1, interleave_z("1c", 1, turn_back(zT1[3:], 3), on_vector))
+        for j in range(3):
+            project(out_a[j], pairs[j], 1, *z1_a)
+        for j in range(2):
+            project(out_b[j], triples[j], 1, *z1_b)
+        store(out_a, 0, HALF, [on_scalar] * 3)
         out_c = [bank(k) for k in (2, 4)]
-        project(out_c, 0, P, chunk(z01[0], 1), chunk(z01[1], 1))
-        project(out_c, 1, P, zc[0][:], zc[1][:])
-        store(out_c, 3 * P, P, (S_, V_))
+        for j in range(2):
+            project(out_c[j], triples[j], 0, *z0_c)
+        store(out_b, 2 * P, P, [on_scalar] * 2)
+        for j in range(2):
+            project(out_c[j], triples[j], 1, *z1_c)
+        store(out_c, 3 * P, P, [on_scalar, on_vector])

from contextlib import ExitStack

import concourse.mybir as mybir

T, S, M, K, H, N = 4096, 1024, 512, 512, 1024, 768
FLOPS = 2 * K * H * S * 2 + 2 * H * N * M

F32 = mybir.dt.float32
BF16 = mybir.dt.bfloat16
I32 = mybir.dt.int32
U32 = mybir.dt.uint32
U16 = mybir.dt.uint16
U8 = mybir.dt.uint8
FP8X4 = mybir.dt.float8_e4m3fn_x4
FP4X4 = mybir.dt.float4_e2m1fn_x4
MULT = mybir.AluOpType.mult
COPY = mybir.ActivationFunctionType.Copy

P = 128
BANK = 512
HALF = 256
PIECE = 1024
GROUPS = 8
H_TILES = 6
KB = 1024

AT_TABLE = 0
AT_WB_SCALES_0 = 16 * KB
AT_WB_ORDERED = 18 * KB
AT_ZEROS = AT_WB_SCALES_0 - 256
ZEROS_COLUMNS = 5 * P
AT_FLOATS = 20 * KB
AT_WB_SCALES_1 = 64 * KB
AT_WA_FIRST = 65 * KB
AT_WB_WORDS = AT_WB_SCALES_1 - 512
AT_H_FIRST = AT_WB_SCALES_1 + 512


def tile_list_latent_key_rebuild_kernel(
    tc, tab_words, tab_scales, offs, offs2, wa, wb_words, wb_scales, wgt, cosm, sinm, wo_words, wo_scales, out
):
    nc = tc.nc
    with ExitStack() as ctx:
        keep = ctx.enter_context(tc.tile_pool(name="keep", bufs=1))
        reuse = ctx.enter_context(tc.tile_pool(name="reuse", bufs=1))
        ring = ctx.enter_context(tc.tile_pool(name="ring", bufs=H_TILES))
        psum = ctx.enter_context(tc.psum_pool(name="psum", bufs=1))

        def held(name, shape, dtype, tag=None):
            return keep.tile(shape, dtype, name=name, tag=tag or name, align_bytes=64)

        def placed(name, shape, dtype, offset):
            return reuse.tile(shape, dtype, name=name, align_bytes=64, offset=offset)

        def chunk(x, c):
            return x[:, P * c : P * (c + 1)]

        def bank(k):
            return psum.tile([P, BANK], F32, name="bank%d" % k)

        def scale_rows(plane, q):
            return plane[32 * q : 32 * q + 4]

        on_scalar, on_vector = nc.scalar.copy, nc.vector.tensor_copy

        offs_t = keep.tile([P, S // 16], U16, name="offs_t")
        offs2_t = keep.tile([P, M // 16], U16, name="offs2_t")
        zeros = placed("zeros", [P, ZEROS_COLUMNS], F32, AT_ZEROS)
        tab_s = held("tab_s", [P, T], U8)
        wb_w = placed("wb_w", [P, 2 * H], U8, AT_WB_WORDS)
        ident = held("ident", [P, P], F32)

        nc.vector.memset(tab_s[:].bitcast(I32), 0)
        nc.gpsimd.memset(zeros[:, :P], 0.0)
        nc.gpsimd.affine_select(
            out=ident[:],
            in_=zeros[:, :P],
            compare_op=mybir.AluOpType.not_equal,
            fill=1.0,
            base=0,
            pattern=[[-1, P]],
            channel_multiplier=1,
        )
        wb_s = [placed("wb_s0", [P, BANK], U8, AT_WB_SCALES_0)]
        nc.vector.memset(wb_s[0][:].bitcast(I32), 0)

        tab_rows = tab_words[0].rearrange("p t i -> p (t i)").bitcast(I32)
        wa_rows = wa.rearrange("(p j) r -> p j r", j=4)
        cos_rows = cosm.rearrange("(b p i) m -> b p i m", b=2, i=4)
        sin_rows = sinm.rearrange("(b p i) m -> b p i m", b=2, i=4)

        nc.sync.dma_start(offs_t[:], offs)
        nc.sync.dma_start(offs2_t[:], offs2)
        nc.sync.dma_start(wb_w[:].bitcast(I32), wb_words[0].bitcast(I32))
        for q in range(4):
            nc.sync.dma_start(scale_rows(tab_s, q).bitcast(I32), tab_scales[0, 4 * q : 4 * q + 4, :].bitcast(I32))
        tab_w = placed("tab_w", [P, T], U32, AT_TABLE)
        nc.sync.dma_start(tab_w[:].bitcast(I32), tab_rows)

        def load_wb_scales(b):
            for q in range(4):
                nc.sync.dma_start(
                    scale_rows(wb_s[b], q).bitcast(I32),
                    wb_scales[0, 4 * q : 4 * q + 4, BANK * b : BANK * (b + 1)].bitcast(I32),
                )

        load_wb_scales(0)

        wbp_w = placed("wbp_w", [P, 2 * H], U8, AT_WB_ORDERED)
        wbp_s = held("wbp_s", [P, H], U8)
        nc.vector.tensor_copy(
            wbp_w[:].bitcast(U16).rearrange("k (b i p) -> k b i p", b=2, i=4),
            wb_w[:].bitcast(U16).rearrange("k (b p i) -> k b i p", b=2, i=4),
        )

        pieces = [placed("wa_first", [P, PIECE], F32, AT_WA_FIRST)[:]]
        wb_s.append(placed("wb_s1", [P, BANK], U8, AT_WB_SCALES_1))
        nc.vector.memset(wb_s[1][:].bitcast(I32), 0)
        floats = placed("floats", [P, 11 * PIECE], F32, AT_FLOATS)
        pieces.extend(floats[:, PIECE * j : PIECE * (j + 1)] for j in range(11))
        wa_raw = [[pieces[2 * b + u].rearrange("k (j r) -> k j r", j=4) for u in range(2)] for b in range(2)]
        sin_t = [[pieces[4 + 2 * b + u].rearrange("p (i m) -> p i m", i=2) for u in range(2)] for b in range(2)]
        cos_0 = [pieces[8 + u].rearrange("p (i m) -> p i m", i=2) for u in range(2)]
        cos_1_late = pieces[10].rearrange("p (i m) -> p i m", i=4)
        wgt_t = pieces[11][:, :M]

        def load_planes(tiles, rows, u):
            nc.sync.dma_start(tiles[u], rows[:, 2 * u : 2 * u + 2, :])

        def load_wa(b):
            for u in range(2):
                nc.sync.dma_start(wa_raw[b][u], wa_rows[:, :, BANK * b + HALF * u : BANK * b + HALF * (u + 1)])

        load_wa(0)
        load_planes(sin_t[0], sin_rows[0], 0)
        load_wb_scales(1)
        load_planes(sin_t[0], sin_rows[0], 1)
        nc.sync.dma_start(wgt_t, wgt)
        load_planes(cos_0, cos_rows[0], 0)
        load_planes(cos_0, cos_rows[0], 1)
        load_planes(sin_t[1], sin_rows[1], 0)
        load_wa(1)
        load_planes(sin_t[1], sin_rows[1], 1)

        v_s = held("v_s", [P, S], U8)
        nc.vector.tensor_copy(v_s[:], tab_s[:].indirect(offs_t[:]))
        wo_s = held("wo_s", [P, 2, N], U8, "tab_s")
        nc.vector.memset(wo_s[:].rearrange("p b n -> p (b n)").bitcast(I32), 0)
        v_w = [held("v_w0", [P, BANK], U32)]

        def order_wb_scales(b):
            nc.vector.tensor_copy(
                wbp_s[:, BANK * b : BANK * (b + 1)].rearrange("k (i p) -> k i p", i=4),
                wb_s[b][:].rearrange("k (p i) -> k i p", i=4),
            )

        wa_w = [held("wa_w%d" % b, [P, BANK], U32) for b in range(2)]
        wa_s = [held("wa_s%d" % b, [P, BANK], U8) for b in range(2)]
        wa_bf = [held("wa_bf%d" % b, [P, 4 * BANK], BF16) for b in range(2)]

        def round_wa_on_scalar(b, u):
            nc.scalar.copy(
                wa_bf[b][:].rearrange("k (i p j) -> k p j i", i=4, j=4)[:, 64 * u : 64 * (u + 1)],
                wa_raw[b][u].rearrange("k j (p i) -> k p j i", i=4),
            )

        def quantise_wa(b):
            nc.vector.quantize_mx(out=wa_w[b][:].bitcast(FP8X4), scales=wa_s[b][:], in_=wa_bf[b][:])

        def product(lhsT, lhsT_scale, first_bank, h):
            for c in range(2):
                acc = bank(first_bank + c)
                nc.tensor.matmul_mx(
                    out=acc[:],
                    lhsT=lhsT,
                    lhsT_scale=lhsT_scale,
                    rhs=v_w[c][:].bitcast(FP8X4),
                    rhs_scale=v_s[:, BANK * c : BANK * (c + 1)],
                    start=True,
                    stop=True,
                )
                nc.scalar.copy(h[:, BANK * c : BANK * (c + 1)], acc[:])
            return h

        def next_h():
            return ring.tile([P, S], F32, name="h")

        def pick(x, h, angle, first_chunk, chunks):
            offsets = offs2_t[:, 8 * first_chunk : 8 * (first_chunk + chunks)]
            nc.vector.tensor_tensor(x, h[:].indirect(offsets), angle, MULT)

        def sine_part(b, i, h):
            c0 = P * (4 * b + i)
            product(wbp_w[:, 2 * c0 : 2 * (c0 + P)].bitcast(FP4X4), wbp_s[:, c0 : c0 + P], 2 * (i % 2), h)
            x = held("xs%d%d" % (b, i), [P, M], F32)
            pick(x[:], h, sin_t[b][i // 2][:, i % 2, :], 0, 4)
            return x

        def cosine_product(b, i, first_bank):
            return product(chunk(wa_w[b], i).bitcast(FP8X4), chunk(wa_s[b], i), first_bank, next_h())

        def cosine_part_0(i):
            h = cosine_product(0, i, 2 * (i % 2))
            x = held("xc%d" % i, [P, M], F32)
            pick(x[:], h, cos_0[i // 2][:, i % 2, :], 0, 4)
            return x

        wgt_T = held("wgt_T", [P, 4 * GROUPS], F32)

        def turn_wgt():
            turned = bank(4)
            for c in range(4):
                nc.tensor.transpose(chunk(turned, c), chunk(wgt_t, c), ident[:])
            nc.scalar.copy(wgt_T[:], turned[:, ::16])

        def add_turned(y, i, x, first=False, last=False):
            nc.tensor.matmul(chunk(y, i), x, ident[:], start=first, stop=last, is_transpose=True)

        def weigh_on_vector(b, c, y):
            zT = held("zT%d%d" % (b, c), [P, BANK], BF16)
            nc.vector.tensor_tensor(
                zT[:].rearrange("m (u p e) -> m u p e", u=2, e=2),
                y[:].rearrange("m (u e p) -> m u p e", u=2, e=2),
                wgt_T[:, GROUPS * c : GROUPS * (c + 1)].unsqueeze(1).unsqueeze(3).to_broadcast([P, 2, GROUPS, 32]),
                MULT,
            )
            return zT

        def weigh_on_scalar(b, c, y):
            zT = held("zT%d%d" % (b, c), [P, BANK], BF16)
            dst = zT[:].rearrange("m (u g s e) -> m g u s e", u=2, g=GROUPS, e=2)
            src = y[:].rearrange("m (u e g s) -> m g u s e", u=2, e=2, g=GROUPS)
            for g in range(GROUPS):
                column = GROUPS * c + g
                nc.scalar.activation(dst[:, g], src[:, g], COPY, scale=wgt_T[:, column : column + 1])
            return zT

        def turn_words(back, slot, zT):
            words = zT[:].bitcast(F32)
            for u in range(2):
                nc.tensor.transpose(chunk(back, 2 * slot + u), chunk(words, u), ident[:])

        def turn_back(zTs, k):
            back = bank(k)
            for slot, zT in enumerate(zTs):
                turn_words(back, slot, zT)
            return back

        def interleave_z(name, chunks, back, copy):
            z = held("z" + name, [P, 4 * P * chunks], BF16)
            copy(
                z[:].bitcast(F32).rearrange("p (c m u) -> p c m u", c=chunks, u=2),
                back[:, : 2 * P * chunks].rearrange("p (c u m) -> p c m u", c=chunks, u=2),
            )
            return z

        def quantise_z(name, chunks, z):
            z_w = held("z_w" + name, [P, P * chunks], U32)
            z_s = held("z_s" + name, [P, P * chunks], U8)
            nc.vector.quantize_mx(out=z_w[:].bitcast(FP8X4), scales=z_s[:], in_=z[:])
            return z_w[:], z_s[:]

        out_rows = out.rearrange("(c p) m -> p c m", p=P)

        def project(acc, row_tiles, b, z_w, z_s):
            width = z_w.shape[1]
            for slot, n in enumerate(row_tiles):
                nc.tensor.matmul_mx(
                    out=acc[:, width * slot : width * (slot + 1)],
                    lhsT=chunk(wo_w[b], n).bitcast(FP8X4),
                    lhsT_scale=chunk(wo_s[:, b, :], n),
                    rhs=z_w.bitcast(FP8X4),
                    rhs_scale=z_s,
                    start=(b == 0 and slot == 0),
                    stop=(b == 1 and slot == len(row_tiles) - 1),
                )

        def store(accs, m0, width, copies):
            per = N // P // len(accs)
            for j, acc in enumerate(accs):
                res = held("res%d_%d" % (m0, j), [P, per * width], F32)
                copies[j](res[:], acc[:, : per * width])
                nc.sync.dma_start(
                    out_rows[:, per * j : per * (j + 1), m0 : m0 + width], res[:].rearrange("p (c m) -> p c m", c=per)
                )

        nc.vector.tensor_copy(v_w[0][:], tab_w[:].indirect(offs_t[:, :32]))
        order_wb_scales(0)
        v_w.append(placed("v_w1", [P, BANK], U32, AT_WB_SCALES_0))
        nc.vector.tensor_copy(v_w[1][:], tab_w[:].indirect(offs_t[:, 32:]))
        cos_1_early = placed("cos_1_early", [P, 4, HALF], F32, AT_TABLE)
        nc.sync.dma_start(cos_1_early[:], cos_rows[1, :, :, :HALF])
        nc.sync.dma_start(cos_1_late, cos_rows[1, :, :, HALF:])
        round_wa_on_scalar(0, 0)
        nc.vector.tensor_copy(
            wa_bf[0][:].rearrange("k (a e p j) -> k a p j e", a=2, e=2, j=4)[:, :, 64:],
            wa_raw[0][1].rearrange("k j (p a e) -> k a p j e", a=2, e=2),
        )
        quantise_wa(0)
        wo_both = held("wo_w", [P, 2 * N], U32, "wa_bf0")
        wo_w = [wo_both[:, N * b : N * (b + 1)] for b in range(2)]
        nc.sync.dma_start(
            wo_both[:].bitcast(I32).rearrange("p (b n) -> p b n", b=2),
            wo_words.rearrange("b p n i -> p b (n i)").bitcast(I32),
        )
        for q in range(4):
            nc.sync.dma_start(
                scale_rows(wo_s, q).bitcast(I32),
                wo_scales[:, 4 * q : 4 * q + 4, :].rearrange("b r n -> r b n").bitcast(I32),
            )

        xs0 = [sine_part(0, i, placed("h_first%d" % i, [P, S], F32, AT_H_FIRST + 4 * KB * i)) for i in range(2)]
        xs0.extend(sine_part(0, i, next_h()) for i in range(2, 4))
        order_wb_scales(1)
        turn_wgt()
        xc0 = [cosine_part_0(i) for i in range(4)]

        xs1 = [sine_part(1, i, next_h()) for i in range(2)]
        for u in range(2):
            round_wa_on_scalar(1, u)
        quantise_wa(1)

        def join_0(c):
            y = bank(4 + c)
            for i in reversed(range(4)):
                add_turned(y, i, chunk(xc0[i], c), first=True)
                add_turned(y, i, chunk(xs0[i], c), last=True)
            return weigh_on_vector(0, c, y)

        early = held("early", [P, 4, HALF], F32)
        ha1 = []

        def early_part(i, first_bank):
            ha1.append(cosine_product(1, i, first_bank))
            pick(early[:, i, :], ha1[i], cos_1_early[:, i, :], 0, 2)

        zT0 = [join_0(0)]
        xs1.extend(sine_part(1, i, next_h()) for i in range(2, 4))
        zT0.append(join_0(1))
        early_part(0, 0)
        zT0.append(join_0(2))
        early_part(1, 2)
        zT0.append(join_0(3))
        early_part(2, 4)
        early_part(3, 0)

        def open_sum(c, k):
            y = bank(k)
            for i in range(4):
                add_turned(y, i, chunk(xs1[i], c), first=(i == 0))
            return y

        def add_early(planes):
            for i in planes:
                for c in range(2):
                    add_turned(y1[c], i, chunk(early[:, i, :], c), last=(i == 3))

        z0_a = quantise_z("0a", 2, interleave_z("0a", 2, turn_back(zT0[:2], 6), on_scalar))
        y1 = [open_sum(c, 2 + c) for c in range(2)]
        add_early(range(2))
        z0_bc_bf = interleave_z("0bc", 2, turn_back(zT0[2:], 7), on_scalar)
        add_early(range(2, 4))
        zT1 = [weigh_on_scalar(1, c, y1[c]) for c in range(2)]
        y1.extend(open_sum(c, 4 + c) for c in range(2, 4))
        back_a = bank(1)
        turn_words(back_a, 0, zT1[0])
        late_b = placed("late_b", [P, 4, P], F32, AT_TABLE)
        for i in range(4):
            pick(late_b[:, i, :], ha1[i], cos_1_late[:, i, :P], 2, 1)
            add_turned(y1[2], i, late_b[:, i, :], last=(i == 3))
        z0_bc = quantise_z("0bc", 2, z0_bc_bf)
        z0_b, z0_c = [(chunk(z0_bc[0], c), chunk(z0_bc[1], c)) for c in range(2)]
        zT1.append(weigh_on_vector(1, 2, y1[2]))

        pairs = [range(2 * j, 2 * j + 2) for j in range(3)]
        triples = [range(3 * j, 3 * j + 3) for j in range(2)]
        out_a = [bank(k) for k in (4, 5, 0)]
        for j in range(2):
            project(out_a[j], pairs[j], 0, *z0_a)
        turn_words(back_a, 1, zT1[1])
        back_b = turn_back(zT1[2:], 2)
        project(out_a[2], pairs[2], 0, *z0_a)
        z1_a_bf = interleave_z("1a", 2, back_a, on_scalar)
        z1_b_bf = interleave_z("1b", 1, back_b, on_scalar)
        out_b = [bank(k) for k in (6, 1)]
        for j in range(2):
            project(out_b[j], triples[j], 0, *z0_b)
        late_c = placed("late_c", [P, 4, P], F32, AT_TABLE)
        for i in range(4):
            pick(late_c[:, i, :], ha1[i], cos_1_late[:, i, P:], 3, 1)
        z1_a = quantise_z("1a", 2, z1_a_bf)
        z1_b = quantise_z("1b", 1, z1_b_bf)
        for i in range(4):
            add_turned(y1[3], i, late_c[:, i, :], last=(i == 3))
        zT1.append(weigh_on_vector(1, 3, y1[3]))
        z1_c = quantise_z("1c", 1, interleave_z("1c", 1, turn_back(zT1[3:], 3), on_vector))
        for j in range(3):
            project(out_a[j], pairs[j], 1, *z1_a)
        for j in range(2):
            project(out_b[j], triples[j], 1, *z1_b)
        store(out_a, 0, HALF, [on_scalar] * 3)
        out_c = [bank(k) for k in (2, 4)]
        for j in range(2):
            project(out_c[j], triples[j], 0, *z0_c)
        store(out_b, 2 * P, P, [on_scalar] * 2)
        for j in range(2):
            project(out_c[j], triples[j], 1, *z1_c)
        store(out_c, 3 * P, P, [on_scalar, on_vector])
